import numpy as np
import ml_dtypes


def mxq(x, axis, fmt="e4m3"):
    dtype, down = {"e4m3": (ml_dtypes.float8_e4m3fn, 7), "e5m2": (ml_dtypes.float8_e5m2, 14)}[fmt]
    v = np.moveaxis(np.asarray(x, np.float32).astype(ml_dtypes.bfloat16).astype(np.float64), axis, -1)
    blocks = v.reshape(v.shape[:-1] + (-1, 32))
    amax = np.abs(blocks).max(-1, keepdims=True)
    byte = np.maximum(np.where(amax > 0, np.frexp(amax)[1] - 1 + 127, 0) - down, 1)
    scale = np.exp2(byte - 127.0)
    codes = (blocks / scale).astype(np.float32).astype(dtype).astype(np.float64)
    return np.moveaxis((codes * scale).reshape(v.shape), -1, axis)


WIDE = False


def mx_kscale(k):
    if not WIDE:
        return np.ones(k)
    levels = np.array([10, -10, 5, -5, 0])
    if k % 512:
        return np.exp2(np.random.permutation(np.resize(levels, k // 32))).repeat(32)
    a = np.empty((k // 512, 16))
    for p in range(k // 512):
        a[p, :8] = np.random.permutation(np.resize(levels, 8))
        for g in range(8):
            far = levels[np.abs(levels - a[p, g]) >= 10]
            a[p, g + 8] = far[np.random.randint(len(far))]
    return np.exp2(a.ravel()).repeat(32)


BF16 = ml_dtypes.bfloat16


def bf(x):
    return np.asarray(x, np.float32).astype(BF16)


def f64(x):
    return np.asarray(x).astype(np.float64)


E2M1 = np.array([0.0, 0.5, 1.0, 1.5, 2.0, 3.0, 4.0, 6.0, -0.0, -0.5, -1.0, -1.5, -2.0, -3.0, -4.0, -6.0])


def pack_weight(w, fmt):
    k, n = w.shape
    w = f64(bf(w)).reshape(k // 32, 32, n)
    amax = np.abs(w).max(1)
    if fmt == "e4m3":
        byte = np.frexp(amax)[1] - 1 + 127 - 7
    else:
        mant, ex = np.frexp(amax / 6.0)
        byte = np.where(mant > 0.5, ex, ex - 1) + 127
    byte = np.clip(np.where(amax > 0, byte, 1), 1, 254)
    scaled = (w * np.exp2(127.0 - byte)[:, None, :]).reshape(k, n).astype(np.float32)
    by_word = np.ascontiguousarray(scaled.reshape(k // 512, 128, 4, n).transpose(0, 1, 3, 2))
    if fmt == "e4m3":
        words = by_word.astype(ml_dtypes.float8_e4m3fn).view(np.uint8)
    else:
        c = by_word.astype(ml_dtypes.float4_e2m1fn).view(np.uint8) & 0xF
        words = c[..., 0::2] | (c[..., 1::2] << 4)
    return np.ascontiguousarray(words), np.ascontiguousarray(byte.astype(np.uint8).reshape(k // 512, 16, n))


def unpack_weight(words, scales, fmt):
    g, p, n, _ = words.shape
    if fmt == "e4m3":
        vals = np.ascontiguousarray(words).view(ml_dtypes.float8_e4m3fn).astype(np.float64)
    else:
        nib = np.empty((g, p, n, 4), np.uint8)
        nib[..., 0::2] = words & 0xF
        nib[..., 1::2] = words >> 4
        vals = E2M1[nib]
    vals = vals * np.repeat(np.exp2(scales.astype(np.float64) - 127.0), 8, axis=1)[..., None]
    return vals.transpose(0, 1, 3, 2).reshape(g * 512, n)
def pack4(w):
    words, scales = pack_weight(w, "e2m1")
    return words.reshape(words.shape[0], 128, -1), scales


def unpack4(words, scales):
    return unpack_weight(words.reshape(words.shape[0], 128, -1, 2), scales, "e2m1")


E4M3FN = np.array([(-1.0 if i & 128 else 1.0) * ((1.0 + (i & 7) / 8.0) * 2.0 ** (((i >> 3) & 15) - 7) if i & 120 else (i & 7) * 2.0 ** -9) for i in range(256)])


def e4m3fn_bytes(y):
    return np.clip(np.asarray(y, np.float64), -448.0, 448.0).astype(np.float32).astype(ml_dtypes.float8_e4m3fn).view(np.uint8)


def e4m3fn_values(b):
    return E4M3FN[b]


N, D, M, T = 2048, 512, 1024, 512

LAM = 64.0


def leaf_score(grad, hess):
    return grad * grad / (hess + LAM)


def draw0():
    u, t = mx_kscale(D), mx_kscale(N)
    x = bf(np.random.standard_normal((N, D)) * u)
    p_words, p_scales = pack4(np.random.standard_normal((D, M)) * 2.0 / np.sqrt(D) / u[:, None])
    b = bf(np.random.standard_normal(M) * 0.5)
    w = bf((1.0 + 0.1 * np.random.standard_normal(N)) * t)
    g = bf(np.random.standard_normal((N, T)) * 90.0 / np.sqrt(N) / t[:, None])
    h = bf(np.random.uniform(1.0 / 3.0, 5.0 / 3.0, N) * 48.0 * LAM / N)
    return {"x": x, "p_words": p_words, "p_scales": p_scales, "b": b, "w": w, "g": g, "h": h}


def core(x, p_words, p_scales, b, w, g, h):
    w64, g64, h64 = f64(w), f64(g), f64(h)
    z = (mxq(f64(x), 1, "e4m3") @ unpack4(p_words, p_scales)) + f64(b)[None, :]
    s = np.tanh(z / 2.0)
    d = mxq((s * w64[:, None]).T, 1, "e4m3") @ mxq(g64, 0, "e4m3")
    gt = np.sum(w64[:, None] * g64, axis=0)
    hd = np.sum(s * h64[:, None], axis=0)
    ht = np.sum(h64)
    GL = (gt[None, :] - d) / 2.0
    GR = (gt[None, :] + d) / 2.0
    HL = ((ht - hd) / 2.0)[:, None]
    HR = ((ht + hd) / 2.0)[:, None]
    return 0.5 * (leaf_score(GL, HL) + leaf_score(GR, HR) - leaf_score(gt[None, :], ht))


def setup_inputs():
    drawn = draw0()
    full = np.asarray(drawn['x']).astype(np.float64)
    scale = (np.abs(full).reshape(2048, 4, 128).max(axis=(2,)) / 448.0).astype(np.float32)
    given = {}
    for key, value in drawn.items():
        if key == 'x':
            given['x_bytes'] = e4m3fn_bytes(full / np.repeat(scale.astype(np.float64), 128, axis=1))
            given['x_scale'] = scale
        else:
            given[key] = value
    return given


def reference(x_bytes, x_scale, p_words, p_scales, b, w, g, h):
    return core(e4m3fn_values(x_bytes) * np.repeat(x_scale.astype(np.float64), 128, axis=1), p_words, p_scales, b, w, g, h)

@@ -1,0 +1,540 @@
+from contextlib import ExitStack
+
+import concourse.mybir as mybir
+from concourse.masks import make_identity
+
+N, D, M, T = 2048, 512, 1024, 512
+P = 128
+NG = N // 512
+NM = M // P
+LAM = 64.0
+FLOPS = 2 * N * D * M + 2 * N * M * T + 2 * N * T + 2 * N * M
+
+F32 = mybir.dt.float32
+BF16 = mybir.dt.bfloat16
+U32 = mybir.dt.uint32
+I32 = mybir.dt.int32
+U8 = mybir.dt.uint8
+FP8 = mybir.dt.float8_e4m3fn
+FP8X4 = mybir.dt.float8_e4m3fn_x4
+FP4X4 = mybir.dt.float4_e2m1fn_x4
+ALU = mybir.AluOpType
+ACT = mybir.ActivationFunctionType
+AX = mybir.AxisListType
+
+
+def tile_obliquesoftsplitgaintable_d1p_kernel(tc, x_bytes, x_scale, p_words, p_scales, b, w, g, h, out):
+    nc = tc.nc
+    V, S, PE = nc.vector, nc.scalar, nc.tensor
+    with ExitStack() as ctx:
+        keep = ctx.enter_context(tc.tile_pool(name="keep", bufs=1))
+        work = ctx.enter_context(tc.tile_pool(name="work", bufs=2))
+        psum = ctx.enter_context(tc.psum_pool(name="psum", bufs=2))
+        ctx.enter_context(tc.manual_schedule())
+
+        def kt(shape, dt, name):
+            return keep.tile(shape, dt, name=name, align_bytes=64)
+
+        ident_f = kt([P, P], F32, "ident_f")
+        ident_b = kt([P, P], BF16, "ident_b")
+        xs = kt([P, NG, 16], F32, "xs")
+        xr = [kt([P, 2048], U8, "xr%d" % i) for i in range(NG)]
+        xq = kt([P, NG, 512], U32, "xq")
+        xqs = kt([P, NG, 512], U8, "xqs")
+        pw = kt([P, 2048], U8, "pw")
+        psc = kt([P, M], U8, "psc")
+        rows = kt([P, 640], BF16, "rows")
+        wh = kt([P, 8, 4], BF16, "wh")
+        hb = kt([P, 8], F32, "hb")
+        h_all = kt([P, 2048], BF16, "h_all")
+        ht4 = kt([P, 4], F32, "ht4")
+        sc = kt([P, 8], F32, "sc")
+        graw = [kt([P, 4, T], BF16, "graw%d" % i) for i in range(NG)]
+        gq = kt([P, NG, T], U32, "gq")
+        gqs = kt([P, NG, T], U8, "gqs")
+        gtn = kt([P, T], F32, "gtn")
+        erow = kt([P, T], F32, "erow")
+        gt2 = kt([P, T], F32, "gt2")
+        warm = kt([P, 1], F32, "warm")
+        half = kt([P, 1], F32, "half")
+        h_f = kt([P, 16], F32, "h_f")
+        root = [kt([P, 1], F32, "root%d" % i) for i in range(NM)]
+        junk = kt([P, 2048], BF16, "junk")
+        swq = [kt([P, 512], U32, "swq%d" % i) for i in range(NM)]
+        sws = [kt([P, 512], U8, "sws%d" % i) for i in range(NM)]
+        hd = [kt([P, 8], F32, "hd%d" % i) for i in range(NM)]
+        st = {}
+
+        xv = x_bytes.rearrange("(G r t) k -> G r (t k)", r=P, t=4)
+        gv = g.rearrange("(G p t) n -> G p t n", p=P, t=4)
+        nc.sync.dma_start(out=xr[0][:], in_=xv[0])
+        nc.scalar.dma_start(out=xs[:], in_=x_scale.rearrange("(G r t) j -> r G (t j)", r=P, t=4))
+        V.memset(rows[:], 0.0)
+        V.memset(psc[:].bitcast(I32), 0)
+        nc.scalar.dma_start(out=rows[0:4, 0:512], in_=w.rearrange("(G f) -> G f", G=4))
+        nc.scalar.dma_start(out=rows[4:8, 0:512], in_=h.rearrange("(G f) -> G f", G=4))
+        nc.scalar.dma_start(out=rows[0:8, 512:640], in_=b.rearrange("(c p) -> c p", p=P))
+        for q in range(4):
+            nc.scalar.dma_start(out=psc[32 * q:32 * q + 4, :].bitcast(I32), in_=p_scales[0, 4 * q:4 * q + 4, :].bitcast(I32))
+        nc.sync.dma_start(out=xr[1][:], in_=xv[1])
+        nc.sync.dma_start(out=pw[:].bitcast(I32), in_=p_words[0].bitcast(I32))
+        for G in range(2, NG):
+            nc.sync.dma_start(out=xr[G][:], in_=xv[G])
+        for G in range(NG):
+            nc.sync.dma_start(out=graw[G][:], in_=gv[G])
+        make_identity(nc, ident_f[:])
+        make_identity(nc, ident_b[:])
+        nc.gpsimd.memset(warm[:], 0.0)
+        nc.gpsimd.memset(half[:], 0.5)
+        S.activation(out=warm[:], in_=warm[:], func=ACT.Tanh)
+
+        def xprod(G, t, eng, js=(0, 1, 2, 3)):
+            if ("xb", G) not in st:
+                st["xb", G] = work.tile([P, 4, 512], BF16, name="xb", bufs=4, align_bytes=64)
+            xb = st["xb", G]
+            for j in js:
+                o = xb[:, t, 128 * j:128 * (j + 1)]
+                i = xr[G][:, 512 * t + 128 * j:512 * t + 128 * (j + 1)].bitcast(FP8)
+                s1 = xs[:, G, 4 * t + j:4 * t + j + 1]
+                if eng == "V":
+                    V.tensor_scalar(out=o, in0=i, scalar1=s1, scalar2=None, op0=ALU.mult)
+                else:
+                    S.activation(out=o, in_=i, func=ACT.Copy, scale=s1)
+
+        def xturn(G, a):
+            t_ps = psum.tile([P, 2, 2, P], F32, name="turn", tag="d", bufs=2)
+            st["xt", G, a] = t_ps
+            for i in range(2):
+                words = st["xb", G][:, 2 * a + i, :].bitcast(F32)
+                for u in range(2):
+                    PE.transpose(t_ps[:, i, u, :], words[:, u:256:2], ident_f[:])
+
+        def xcopy(G, a, eng):
+            if ("gx", G) not in st:
+                st["gx", G] = work.tile([P, 2048], BF16, name="gx", bufs=3, align_bytes=64)
+            o = st["gx", G][:, 1024 * a:1024 * (a + 1)].bitcast(F32).rearrange("p (i r u) -> p i r u", i=2, u=2)
+            i = st["xt", G, a][:].rearrange("p i u r -> p i r u")
+            if eng == "V":
+                V.tensor_copy(out=o, in_=i)
+            else:
+                S.copy(out=o, in_=i)
+
+        def xquant(G, c0=0, c1=512):
+            V.quantize_mx(out=xq[:, G, c0:c1].bitcast(FP8X4), scales=xqs[:, G, c0:c1], in_=st["gx", G][:, 4 * c0:4 * c1])
+
+        def gmix(G, eng):
+            gg = work.tile([P, T, 4], BF16, name="gg", bufs=3, align_bytes=64)
+            st["gg", G] = gg
+            if eng == "V":
+                V.tensor_copy(out=gg[:], in_=graw[G][:].rearrange("p t n -> p n t"))
+            else:
+                S.copy(out=gg[:], in_=graw[G][:].rearrange("p t n -> p n t"))
+
+        def gquant(G):
+            V.quantize_mx(out=gq[:, G, :].bitcast(FP8X4), scales=gqs[:, G, :], in_=st["gg", G][:].rearrange("p n t -> p (n t)"))
+
+        def zmul(m, G):
+            z = psum.tile([P, 512], F32, name="z", tag="z", bufs=3)
+            st["z", m, G] = z
+            PE.matmul_mx(out=z[:], lhsT=pw[:, 256 * m:256 * (m + 1)].bitcast(FP4X4), lhsT_scale=psc[:, P * m:P * (m + 1)],
+                         rhs=xq[:, G, :].bitcast(FP8X4), rhs_scale=xqs[:, G, :], start=True, stop=True)
+
+        def tanh(m, G):
+            if ("s", m) not in st:
+                st["s", m] = work.tile([P, 2048], F32, name="s", bufs=6, align_bytes=64)
+            S.activation(out=st["s", m][:, 512 * G:512 * (G + 1)], in_=st["z", m, G][:], func=ACT.Tanh, bias=hb[:, m:m + 1], scale=0.5)
+
+        def sturn(m, G):
+            t_ps = psum.tile([P, 4, P], F32, name="sturn", tag="tr", bufs=3)
+            st["tr", m, G] = t_ps
+            for t in range(4):
+                PE.transpose(t_ps[:, t, :], st["s", m][:, 512 * G + P * t:512 * G + P * (t + 1)], ident_f[:])
+
+        def smul(m, G):
+            if ("sw", m) not in st:
+                st["sw", m] = work.tile([P, 2048], BF16, name="sw", bufs=6, align_bytes=64)
+            o = st["sw", m][:, 512 * G:512 * (G + 1)].rearrange("p (m t) -> p m t", t=4)
+            V.tensor_tensor(out=o, in0=st["tr", m, G][:].rearrange("p t m -> p m t"),
+                            in1=wh[:, G:G + 1, :].to_broadcast([P, P, 4]), op=ALU.mult)
+
+        def hdiff(m, G0=0, G1=NG):
+            o = hd[m][:, 0:1] if G1 - G0 == NG else hd[m][:, 4 + G0 // 2:5 + G0 // 2]
+            V.scalar_tensor_tensor(out=junk[:, 512 * G0:512 * G1], in0=st["s", m][:, 512 * G0:512 * G1], scalar=1.0, in1=h_all[:, 512 * G0:512 * G1],
+                                   op0=ALU.mult, op1=ALU.mult, accum_out=o)
+
+        def hjoin(m):
+            V.tensor_tensor(out=hd[m][:, 0:1], in0=hd[m][:, 4:5], in1=hd[m][:, 5:6], op=ALU.add)
+
+        def squant(m):
+            V.quantize_mx(out=swq[m][:].bitcast(FP8X4), scales=sws[m][:], in_=st["sw", m][:])
+
+        def alpha1(m):
+            V.tensor_scalar(out=hd[m][:, 1:2], in0=hd[m][:, 0:1], scalar1=sc[:, 3:4], scalar2=2.0, op0=ALU.mult, op1=ALU.add)
+
+        def alpha2(m):
+            V.scalar_tensor_tensor(out=hd[m][:, 2:3], in0=hd[m][:, 0:1], scalar=sc[:, 1:2], in1=hd[m][:, 1:2], op0=ALU.add, op1=ALU.mult)
+
+        def alpha3(m):
+            V.reciprocal(out=hd[m][:, 3:4], in_=hd[m][:, 2:3])
+
+        def dmul(m, cols=((0, T),)):
+            d = psum.tile([P, T], F32, name="d", tag="d", bufs=2)
+            st["d", m] = d
+            for c0, c1 in cols:
+                for G in range(NG):
+                    PE.matmul_mx(out=d[:, c0:c1], lhsT=swq[m][:, P * G:P * (G + 1)].bitcast(FP8X4), lhsT_scale=sws[m][:, P * G:P * (G + 1)],
+                                 rhs=gq[:, G, c0:c1].bitcast(FP8X4), rhs_scale=gqs[:, G, c0:c1], start=(G == 0), stop=(G == NG - 1))
+
+        def tile3(kind, m):
+            if (kind, m) not in st:
+                st[kind, m] = work.tile([P, T], F32, name=kind, bufs=3)
+            return st[kind, m]
+
+        def ushift(m, c0=0, c1=T):
+            V.scalar_tensor_tensor(out=tile3("u", m)[:, c0:c1], in0=gtn[:, c0:c1], scalar=hd[m][:, 0:1], in1=st["d", m][:, c0:c1], op0=ALU.mult, op1=ALU.add)
+
+        def usq(m, c0=0, c1=T):
+            S.activation(out=tile3("q", m)[:, c0:c1], in_=st["u", m][:, c0:c1], func=ACT.Square, scale=root[m][:] if ("root", m) in st else 1.0)
+
+        def aroot(m):
+            st["root", m] = True
+            nc.gpsimd.tensor_tensor(out=root[m][:], in0=hd[m][:, 3:4], in1=half[:], op=ALU.pow)
+
+        def gfin(m):
+            o = tile3("o", m)
+            nc.gpsimd.tensor_tensor(out=o[:], in0=st["q", m][:], in1=erow[:], op=ALU.subtract)
+            nc.sync.dma_start(out=out[P * m:P * (m + 1), :], in_=o[:])
+
+        def hcp(m, G):
+            if ("sT", m) not in st:
+                st["sT", m] = work.tile([P, 2048], F32, name="sT", bufs=2, align_bytes=64)
+            S.copy(out=st["sT", m][:, 512 * G:512 * (G + 1)], in_=st["tr", m, G][:].rearrange("p t m -> p (t m)"))
+
+        def hmul(m):
+            ha = psum.tile([P, 2], F32, name="ha", tag="d", bufs=2)
+            st["ha", m] = ha
+            for i in range(16):
+                PE.matmul(ha[:, 0:1], lhsT=st["sT", m][:, P * i:P * (i + 1)], rhs=h_f[:, i:i + 1], start=(i == 0), stop=(i == 15))
+
+        def hout(m):
+            ha = st["ha", m]
+            V.tensor_copy(out=hd[m][:, 0:1], in_=ha[:, 0:1])
+
+        def fin(m, c0=0, c1=T):
+            o = tile3("o", m)
+            V.scalar_tensor_tensor(out=o[:, c0:c1], in0=st["q", m][:, c0:c1], scalar=hd[m][:, 3:4], in1=erow[:, c0:c1], op0=ALU.mult, op1=ALU.subtract)
+            nc.sync.dma_start(out=out[P * m:P * (m + 1), c0:c1], in_=o[:, c0:c1])
+
+        def turn_rows():
+            t_ps = psum.tile([P, 5, P], BF16, name="rt", tag="d", bufs=2)
+            for t in range(4):
+                PE.transpose(t_ps[:, t, :], rows[:, t:512:4], ident_b[:])
+            PE.transpose(t_ps[:, 4, :], rows[:, 512:640], ident_b[:])
+            st["rt"] = t_ps
+
+        def rows_out():
+            t_ps = st["rt"]
+            V.tensor_copy(out=wh[:], in_=t_ps[:, 0:4, 0:8].rearrange("p t c -> p c t"))
+            V.tensor_copy(out=h_f[:].rearrange("p (c t) -> p c t", t=4), in_=wh[:, 4:8, :])
+            V.tensor_scalar(out=hb[:], in0=t_ps[:, 4, 0:8], scalar1=0.5, scalar2=None, op0=ALU.mult)
+
+        def hspread(G):
+            t_ps = psum.tile([P, 512], F32, name="hs", tag="d", bufs=2)
+            st["hs", G] = t_ps
+            for t in range(4):
+                PE.matmul(t_ps[:, P * t:P * (t + 1)], lhsT=wh[:, 4 + G, t:t + 1].to_broadcast([P, P]), rhs=ident_b[:], start=True, stop=True)
+
+        def hcopy(G):
+            S.activation(out=h_all[:, 512 * G:512 * (G + 1)], in_=st["hs", G][:], func=ACT.Copy, accum_out=ht4[:, G:G + 1])
+
+        def gtotal():
+            t_ps = psum.tile([P, T], F32, name="gt", tag="d", bufs=2)
+            st["gt"] = t_ps
+            for G in range(NG):
+                for t in range(4):
+                    PE.matmul(t_ps[:], lhsT=wh[:, G, t:t + 1].to_broadcast([P, P]), rhs=graw[G][:, t, :], start=(G == 0 and t == 0), stop=(G == NG - 1 and t == 3))
+
+        def totals():
+            V.tensor_reduce(out=sc[:, 0:1], in_=ht4[:], axis=AX.X, op=ALU.add)
+            V.tensor_scalar(out=sc[:, 1:2], in0=sc[:, 0:1], scalar1=2.0 * LAM, scalar2=None, op0=ALU.add)
+            V.reciprocal(out=sc[:, 2:3], in_=sc[:, 1:2])
+            V.tensor_scalar(out=sc[:, 5:6], in0=sc[:, 0:1], scalar1=LAM, scalar2=sc[:, 1:2], op0=ALU.add, op1=ALU.mult)
+            V.tensor_scalar(out=sc[:, 3:4], in0=sc[:, 2:3], scalar1=-2.0, scalar2=None, op0=ALU.mult)
+            V.tensor_scalar(out=sc[:, 4:5], in0=sc[:, 2:3], scalar1=-1.0, scalar2=None, op0=ALU.mult)
+            V.reciprocal(out=sc[:, 6:7], in_=sc[:, 5:6])
+            V.tensor_scalar(out=sc[:, 7:8], in0=sc[:, 6:7], scalar1=0.5 * LAM, scalar2=None, op0=ALU.mult)
+
+        def gt_rows_s():
+            S.activation(out=gt2[:], in_=st["gt"][:], func=ACT.Square)
+            S.activation(out=gtn[:], in_=st["gt"][:], func=ACT.Copy, scale=sc[:, 4:5])
+
+        def gt_rows_v():
+            V.tensor_scalar(out=erow[:], in0=gt2[:], scalar1=sc[:, 7:8], scalar2=None, op0=ALU.mult)
+
+        xprod(0, 2, "V")
+        xprod(0, 3, "S")
+        turn_rows()
+        xprod(0, 0, "V")
+        xprod(0, 1, "V")
+        xturn(0, 1)
+        rows_out()
+        xprod(1, 1, "V")
+        xturn(0, 0)
+        xprod(1, 3, "V")
+        xcopy(0, 1, "S")
+        xprod(2, 0, "V")
+        xprod(1, 2, "V")
+        xcopy(0, 0, "S")
+        hspread(0)
+        xprod(3, 2, "V")
+        xprod(3, 3, "V")
+        hcopy(0)
+        xturn(1, 1)
+        xquant(0, 0, 256)
+        xprod(2, 2, "V")
+        gmix(0, "S")
+        hspread(1)
+        xprod(3, 1, "V")
+        xprod(2, 1, "V")
+        xprod(3, 0, "V")
+        xquant(0, 256, 512)
+        xprod(2, 3, "V")
+        zmul(3, 0)
+        xprod(1, 0, "V")
+        zmul(0, 0)
+        zmul(1, 0)
+        xcopy(1, 1, "S")
+        gquant(0)
+        tanh(1, 0)
+        xturn(1, 0)
+        hcopy(1)
+        sturn(1, 0)
+        xcopy(1, 0, "S")
+        zmul(2, 0)
+        smul(1, 0)
+        xturn(2, 0)
+        tanh(0, 0)
+        xquant(1)
+        xturn(2, 1)
+        tanh(2, 0)
+        xcopy(2, 0, "S")
+        zmul(0, 1)
+        sturn(2, 0)
+        xcopy(2, 1, "S")
+        sturn(0, 0)
+        smul(2, 0)
+        tanh(0, 1)
+        zmul(1, 1)
+        smul(0, 0)
+        xturn(3, 0)
+        tanh(3, 0)
+        xquant(2)
+        sturn(0, 1)
+        tanh(1, 1)
+        sturn(3, 0)
+        hdiff(0, 0, 2)
+        xcopy(3, 0, "S")
+        zmul(0, 2)
+        sturn(1, 1)
+        gmix(3, "S")
+        hspread(3)
+        smul(3, 0)
+        zmul(2, 1)
+        xturn(3, 1)
+        smul(1, 1)
+        smul(0, 1)
+        zmul(4, 2)
+        hdiff(1, 0, 2)
+        tanh(0, 2)
+        tanh(2, 1)
+        sturn(0, 2)
+        gquant(3)
+        zmul(1, 2)
+        xcopy(3, 1, "S")
+        smul(0, 2)
+        zmul(3, 1)
+        tanh(1, 2)
+        sturn(2, 1)
+        xquant(3)
+        hspread(2)
+        tanh(3, 1)
+        sturn(1, 2)
+        smul(2, 1)
+        hcopy(2)
+        zmul(0, 3)
+        smul(1, 2)
+        zmul(1, 3)
+        hcopy(3)
+        sturn(3, 1)
+        hdiff(2, 0, 2)
+        gtotal()
+        tanh(0, 3)
+        tanh(1, 3)
+        smul(3, 1)
+        gmix(2, "S")
+        hdiff(0, 2, 4)
+        totals()
+        hdiff(1, 2, 4)
+        gmix(1, "S")
+        sturn(0, 3)
+        gquant(2)
+        zmul(2, 3)
+        smul(0, 3)
+        zmul(3, 3)
+        sturn(1, 3)
+        hjoin(0); alpha1(0); alpha2(0); alpha3(0)
+        squant(0)
+        tanh(3, 3)
+        aroot(0)
+        smul(1, 3)
+        tanh(2, 3)
+        zmul(4, 1)
+        sturn(3, 3)
+        gquant(1)
+        gt_rows_s()
+        zmul(3, 2)
+        smul(3, 3)
+        sturn(2, 3)
+        dmul(0)
+        hdiff(3, 0, 2)
+        tanh(3, 2)
+        tanh(4, 1)
+        tanh(4, 2)
+        smul(2, 3)
+        zmul(4, 0)
+        sturn(4, 1)
+        tanh(4, 0)
+        ushift(0)
+        zmul(2, 2)
+        zmul(5, 0)
+        smul(4, 1)
+        tanh(2, 2)
+        zmul(4, 3)
+        gt_rows_v()
+        sturn(3, 2)
+        tanh(5, 0)
+        squant(1)
+        sturn(2, 2)
+        usq(0)
+        hdiff(2, 2, 4)
+        zmul(5, 2)
+        dmul(1)
+        tanh(4, 3)
+        gfin(0)
+        tanh(5, 2)
+        smul(2, 2)
+        hcp(4, 1)
+        zmul(5, 3)
+        smul(3, 2)
+        sturn(5, 2)
+        tanh(5, 3)
+        squant(2)
+        sturn(4, 3)
+        sturn(4, 0)
+        squant(3)
+        zmul(6, 1)
+        smul(4, 3)
+        zmul(6, 3)
+        tanh(6, 1)
+        zmul(6, 0)
+        hjoin(2); alpha1(2); alpha2(2); alpha3(2)
+        dmul(2)
+        hcp(4, 3)
+        smul(4, 0)
+        aroot(2)
+        tanh(6, 3)
+        hjoin(1); alpha1(1); alpha2(1); alpha3(1)
+        smul(5, 2)
+        aroot(1)
+        hcp(4, 0)
+        sturn(4, 2)
+        ushift(1)
+        zmul(5, 1)
+        hcp(5, 2)
+        sturn(5, 0)
+        smul(4, 2)
+        usq(1)
+        dmul(3)
+        ushift(2)
+        hcp(4, 2)
+        gfin(1)
+        squant(4)
+        usq(2)
+        sturn(5, 3)
+        hdiff(3, 2, 4)
+        hmul(4)
+        tanh(5, 1)
+        gfin(2)
+        tanh(6, 0)
+        smul(5, 3)
+        hjoin(3); alpha1(3); alpha2(3); alpha3(3)
+        hcp(5, 3)
+        smul(5, 0)
+        aroot(3)
+        sturn(6, 0)
+        hout(4)
+        ushift(3)
+        sturn(5, 1)
+        hcp(5, 0)
+        dmul(4)
+        smul(6, 0)
+        usq(3)
+        smul(5, 1)
+        gfin(3)
+        sturn(6, 1)
+        alpha1(4); alpha2(4); alpha3(4)
+        hcp(5, 1)
+        squant(5)
+        zmul(6, 2)
+        sturn(6, 3)
+        smul(6, 1)
+        tanh(6, 2)
+        aroot(4)
+        hmul(5)
+        smul(6, 3)
+        hdiff(6)
+        zmul(7, 3)
+        zmul(7, 1)
+        tanh(7, 3)
+        zmul(7, 2)
+        hout(5)
+        ushift(4)
+        sturn(6, 2)
+        tanh(7, 1)
+        sturn(7, 3)
+        alpha1(6); alpha2(6); alpha3(6)
+        tanh(7, 2)
+        smul(6, 2)
+        sturn(7, 1)
+        aroot(6)
+        usq(4)
+        zmul(7, 0)
+        alpha1(5); alpha2(5); alpha3(5)
+        smul(7, 1)
+        sturn(7, 2)
+        aroot(5)
+        tanh(7, 0)
+        dmul(5)
+        smul(7, 3)
+        gfin(4)
+        smul(7, 2)
+        squant(6)
+        sturn(7, 0)
+        smul(7, 0)
+        dmul(6)
+        ushift(5)
+        squant(7)
+        usq(5)
+        ushift(6)
+        dmul(7, ((0, 256), (256, 512)))
+        gfin(5)
+        hdiff(7)
+        usq(6)
+        gfin(6)
+        alpha1(7); alpha2(7); alpha3(7)
+        ushift(7, 256, 512)
+        ushift(7, 0, 256)
+        usq(7, 256, 512)
+        usq(7, 0, 256)
+        fin(7, 256, 512)
+        fin(7, 0, 256)

@@ -56,7 +56,7 @@ def tile_obliquesoftsplitgaintable_d1p_kernel(tc, x_bytes, x_scale, p_words, p_s
         erow = kt([P, T], F32, "erow")
         gt2 = kt([P, T], F32, "gt2")
         warm = kt([P, 1], F32, "warm")
-        half = kt([P, 1], F32, "half")
+        pows = kt([P, 2], F32, "pows")
         h_f = kt([P, 16], F32, "h_f")
         root = [kt([P, 1], F32, "root%d" % i) for i in range(NM)]
         junk = kt([P, 2048], BF16, "junk")
@@ -67,13 +67,17 @@ def tile_obliquesoftsplitgaintable_d1p_kernel(tc, x_bytes, x_scale, p_words, p_s
 
         xv = x_bytes.rearrange("(G r t) k -> G r (t k)", r=P, t=4)
         gv = g.rearrange("(G p t) n -> G p t n", p=P, t=4)
-        nc.sync.dma_start(out=xr[0][:], in_=xv[0])
-        nc.scalar.dma_start(out=xs[:], in_=x_scale.rearrange("(G r t) j -> r G (t j)", r=P, t=4))
+        xsv = x_scale.rearrange("(G r t) j -> G r (t j)", r=P, t=4)
+        nc.scalar.dma_start(out=xs[:, 0, :], in_=xsv[0])
+        for t in range(4):
+            nc.sync.dma_start(out=xr[0][:, 512 * t:512 * (t + 1)], in_=xv[0][:, 512 * t:512 * (t + 1)])
         V.memset(rows[:], 0.0)
         V.memset(psc[:].bitcast(I32), 0)
         nc.scalar.dma_start(out=rows[0:4, 0:512], in_=w.rearrange("(G f) -> G f", G=4))
         nc.scalar.dma_start(out=rows[4:8, 0:512], in_=h.rearrange("(G f) -> G f", G=4))
         nc.scalar.dma_start(out=rows[0:8, 512:640], in_=b.rearrange("(c p) -> c p", p=P))
+        for G in range(1, NG):
+            nc.scalar.dma_start(out=xs[:, G, :], in_=xsv[G])
         for q in range(4):
             nc.scalar.dma_start(out=psc[32 * q:32 * q + 4, :].bitcast(I32), in_=p_scales[0, 4 * q:4 * q + 4, :].bitcast(I32))
         nc.sync.dma_start(out=xr[1][:], in_=xv[1])
@@ -85,7 +89,8 @@ def tile_obliquesoftsplitgaintable_d1p_kernel(tc, x_bytes, x_scale, p_words, p_s
         make_identity(nc, ident_f[:])
         make_identity(nc, ident_b[:])
         nc.gpsimd.memset(warm[:], 0.0)
-        nc.gpsimd.memset(half[:], 0.5)
+        nc.gpsimd.memset(pows[:, 0:1], -0.5)
+        nc.gpsimd.memset(pows[:, 1:2], -1.0)
         S.activation(out=warm[:], in_=warm[:], func=ACT.Tanh)
 
         def xprod(G, t, eng, js=(0, 1, 2, 3)):
@@ -168,14 +173,13 @@ def tile_obliquesoftsplitgaintable_d1p_kernel(tc, x_bytes, x_scale, p_words, p_s
         def squant(m):
             V.quantize_mx(out=swq[m][:].bitcast(FP8X4), scales=sws[m][:], in_=st["sw", m][:])
 
-        def alpha1(m):
-            V.tensor_scalar(out=hd[m][:, 1:2], in0=hd[m][:, 0:1], scalar1=sc[:, 3:4], scalar2=2.0, op0=ALU.mult, op1=ALU.add)
-
-        def alpha2(m):
-            V.scalar_tensor_tensor(out=hd[m][:, 2:3], in0=hd[m][:, 0:1], scalar=sc[:, 1:2], in1=hd[m][:, 1:2], op0=ALU.add, op1=ALU.mult)
-
-        def alpha3(m):
-            V.reciprocal(out=hd[m][:, 3:4], in_=hd[m][:, 2:3])
+        def aroot(m, pieces):
+            GP = nc.gpsimd
+            if pieces == 2:
+                GP.tensor_tensor(out=hd[m][:, 0:1], in0=hd[m][:, 4:5], in1=hd[m][:, 5:6], op=ALU.add)
+            GP.tensor_scalar(out=hd[m][:, 1:2], in0=hd[m][:, 0:1], scalar1=sc[:, 3:4], scalar2=2.0, op0=ALU.mult, op1=ALU.add)
+            GP.tensor_scalar(out=hd[m][:, 2:3], in0=hd[m][:, 0:1], scalar1=sc[:, 1:2], scalar2=hd[m][:, 1:2], op0=ALU.add, op1=ALU.mult)
+            GP.tensor_tensor(out=root[m][:], in0=hd[m][:, 2:3], in1=pows[:, 0:1], op=ALU.pow)
 
         def dmul(m, cols=((0, T),)):
             d = psum.tile([P, T], F32, name="d", tag="d", bufs=2)
@@ -194,11 +198,7 @@ def tile_obliquesoftsplitgaintable_d1p_kernel(tc, x_bytes, x_scale, p_words, p_s
             V.scalar_tensor_tensor(out=tile3("u", m)[:, c0:c1], in0=gtn[:, c0:c1], scalar=hd[m][:, 0:1], in1=st["d", m][:, c0:c1], op0=ALU.mult, op1=ALU.add)
 
         def usq(m, c0=0, c1=T):
-            S.activation(out=tile3("q", m)[:, c0:c1], in_=st["u", m][:, c0:c1], func=ACT.Square, scale=root[m][:] if ("root", m) in st else 1.0)
-
-        def aroot(m):
-            st["root", m] = True
-            nc.gpsimd.tensor_tensor(out=root[m][:], in0=hd[m][:, 3:4], in1=half[:], op=ALU.pow)
+            S.activation(out=tile3("q", m)[:, c0:c1], in_=st["u", m][:, c0:c1], func=ACT.Square, scale=root[m][:])
 
         def gfin(m):
             o = tile3("o", m)
@@ -222,7 +222,7 @@ def tile_obliquesoftsplitgaintable_d1p_kernel(tc, x_bytes, x_scale, p_words, p_s
 
         def fin(m, c0=0, c1=T):
             o = tile3("o", m)
-            V.scalar_tensor_tensor(out=o[:, c0:c1], in0=st["q", m][:, c0:c1], scalar=hd[m][:, 3:4], in1=erow[:, c0:c1], op0=ALU.mult, op1=ALU.subtract)
+            V.tensor_tensor(out=o[:, c0:c1], in0=st["q", m][:, c0:c1], in1=erow[:, c0:c1], op=ALU.subtract)
             nc.sync.dma_start(out=out[P * m:P * (m + 1), c0:c1], in_=o[:, c0:c1])
 
         def turn_rows():
@@ -247,22 +247,22 @@ def tile_obliquesoftsplitgaintable_d1p_kernel(tc, x_bytes, x_scale, p_words, p_s
         def hcopy(G):
             S.activation(out=h_all[:, 512 * G:512 * (G + 1)], in_=st["hs", G][:], func=ACT.Copy, accum_out=ht4[:, G:G + 1])
 
-        def gtotal():
-            t_ps = psum.tile([P, T], F32, name="gt", tag="d", bufs=2)
-            st["gt"] = t_ps
-            for G in range(NG):
-                for t in range(4):
-                    PE.matmul(t_ps[:], lhsT=wh[:, G, t:t + 1].to_broadcast([P, P]), rhs=graw[G][:, t, :], start=(G == 0 and t == 0), stop=(G == NG - 1 and t == 3))
+        def gtotal(G):
+            if G == 0:
+                st["gt"] = psum.tile([P, T], F32, name="gt", tag="d", bufs=2)
+            for t in range(4):
+                PE.matmul(st["gt"][:], lhsT=wh[:, G, t:t + 1].to_broadcast([P, P]), rhs=graw[G][:, t, :], start=(G == 0 and t == 0), stop=(G == NG - 1 and t == 3))
 
         def totals():
+            GP = nc.gpsimd
             V.tensor_reduce(out=sc[:, 0:1], in_=ht4[:], axis=AX.X, op=ALU.add)
-            V.tensor_scalar(out=sc[:, 1:2], in0=sc[:, 0:1], scalar1=2.0 * LAM, scalar2=None, op0=ALU.add)
-            V.reciprocal(out=sc[:, 2:3], in_=sc[:, 1:2])
-            V.tensor_scalar(out=sc[:, 5:6], in0=sc[:, 0:1], scalar1=LAM, scalar2=sc[:, 1:2], op0=ALU.add, op1=ALU.mult)
-            V.tensor_scalar(out=sc[:, 3:4], in0=sc[:, 2:3], scalar1=-2.0, scalar2=None, op0=ALU.mult)
-            V.tensor_scalar(out=sc[:, 4:5], in0=sc[:, 2:3], scalar1=-1.0, scalar2=None, op0=ALU.mult)
-            V.reciprocal(out=sc[:, 6:7], in_=sc[:, 5:6])
-            V.tensor_scalar(out=sc[:, 7:8], in0=sc[:, 6:7], scalar1=0.5 * LAM, scalar2=None, op0=ALU.mult)
+            GP.tensor_scalar(out=sc[:, 1:2], in0=sc[:, 0:1], scalar1=1.0, scalar2=2.0 * LAM, op0=ALU.mult, op1=ALU.add)
+            GP.tensor_tensor(out=sc[:, 2:3], in0=sc[:, 1:2], in1=pows[:, 1:2], op=ALU.pow)
+            GP.tensor_scalar(out=sc[:, 3:4], in0=sc[:, 2:3], scalar1=-2.0, scalar2=0.0, op0=ALU.mult, op1=ALU.add)
+            GP.tensor_scalar(out=sc[:, 4:5], in0=sc[:, 2:3], scalar1=-1.0, scalar2=0.0, op0=ALU.mult, op1=ALU.add)
+            GP.tensor_scalar(out=sc[:, 5:6], in0=sc[:, 0:1], scalar1=LAM, scalar2=sc[:, 1:2], op0=ALU.add, op1=ALU.mult)
+            GP.tensor_tensor(out=sc[:, 6:7], in0=sc[:, 5:6], in1=pows[:, 1:2], op=ALU.pow)
+            GP.tensor_scalar(out=sc[:, 7:8], in0=sc[:, 6:7], scalar1=0.5 * LAM, scalar2=0.0, op0=ALU.mult, op1=ALU.add)
 
         def gt_rows_s():
             S.activation(out=gt2[:], in_=st["gt"][:], func=ACT.Square)
@@ -271,268 +271,254 @@ def tile_obliquesoftsplitgaintable_d1p_kernel(tc, x_bytes, x_scale, p_words, p_s
         def gt_rows_v():
             V.tensor_scalar(out=erow[:], in0=gt2[:], scalar1=sc[:, 7:8], scalar2=None, op0=ALU.mult)
 
-        xprod(0, 2, "V")
-        xprod(0, 3, "S")
-        turn_rows()
         xprod(0, 0, "V")
+        xprod(0, 3, "S")
+        xprod(0, 2, "V")
+        turn_rows()
         xprod(0, 1, "V")
-        xturn(0, 1)
-        rows_out()
-        xprod(1, 1, "V")
-        xturn(0, 0)
         xprod(1, 3, "V")
+        xturn(0, 1)
+        xprod(1, 1, "V")
+        rows_out()
+        xprod(1, 2, "V")
+        xturn(0, 0)
+        xprod(2, 3, "V")
         xcopy(0, 1, "S")
         xprod(2, 0, "V")
-        xprod(1, 2, "V")
-        xcopy(0, 0, "S")
-        hspread(0)
-        xprod(3, 2, "V")
-        xprod(3, 3, "V")
-        hcopy(0)
-        xturn(1, 1)
-        xquant(0, 0, 256)
-        xprod(2, 2, "V")
-        gmix(0, "S")
-        hspread(1)
-        xprod(3, 1, "V")
-        xprod(2, 1, "V")
-        xprod(3, 0, "V")
-        xquant(0, 256, 512)
-        xprod(2, 3, "V")
-        zmul(3, 0)
         xprod(1, 0, "V")
-        zmul(0, 0)
-        zmul(1, 0)
-        xcopy(1, 1, "S")
-        gquant(0)
-        tanh(1, 0)
+        xturn(1, 1)
+        xcopy(0, 0, "S")
+        xquant(0, 256, 512)
+        xprod(3, 1, "V")
+        gmix(0, "S")
+        xprod(2, 2, "V")
         xturn(1, 0)
-        hcopy(1)
-        sturn(1, 0)
-        xcopy(1, 0, "S")
+        xquant(0, 0, 256)
+        xprod(2, 1, "V")
         zmul(2, 0)
-        smul(1, 0)
+        xprod(3, 3, "V")
+        zmul(1, 0)
+        xprod(3, 2, "V")
+        zmul(3, 0)
+        xprod(3, 0, "V")
+        xcopy(1, 0, "S")
+        gquant(0)
+        tanh(3, 0)
         xturn(2, 0)
-        tanh(0, 0)
-        xquant(1)
-        xturn(2, 1)
+        xcopy(1, 1, "S")
+        sturn(3, 0)
         tanh(2, 0)
+        xquant(1)
+        zmul(0, 0)
         xcopy(2, 0, "S")
-        zmul(0, 1)
+        xturn(2, 1)
+        smul(3, 0)
+        tanh(0, 0)
         sturn(2, 0)
+        zmul(0, 1)
         xcopy(2, 1, "S")
         sturn(0, 0)
         smul(2, 0)
-        tanh(0, 1)
-        zmul(1, 1)
-        smul(0, 0)
-        xturn(3, 0)
-        tanh(3, 0)
+        tanh(1, 0)
+        hspread(1)
         xquant(2)
+        zmul(1, 1)
+        tanh(0, 1)
+        hspread(0)
+        smul(0, 0)
+        sturn(1, 0)
+        hcopy(1)
         sturn(0, 1)
-        tanh(1, 1)
-        sturn(3, 0)
-        hdiff(0, 0, 2)
-        xcopy(3, 0, "S")
+        hcopy(0)
+        smul(1, 0)
         zmul(0, 2)
-        sturn(1, 1)
-        gmix(3, "S")
-        hspread(3)
-        smul(3, 0)
-        zmul(2, 1)
-        xturn(3, 1)
-        smul(1, 1)
-        smul(0, 1)
-        zmul(4, 2)
-        hdiff(1, 0, 2)
-        tanh(0, 2)
-        tanh(2, 1)
-        sturn(0, 2)
-        gquant(3)
-        zmul(1, 2)
-        xcopy(3, 1, "S")
-        smul(0, 2)
         zmul(3, 1)
-        tanh(1, 2)
-        sturn(2, 1)
-        xquant(3)
+        tanh(1, 1)
+        smul(0, 1)
         hspread(2)
-        tanh(3, 1)
-        sturn(1, 2)
-        smul(2, 1)
+        hspread(3)
+        tanh(0, 2)
+        hdiff(0, 0, 2)
+        sturn(1, 1)
         hcopy(2)
-        zmul(0, 3)
+        zmul(2, 1)
+        zmul(1, 2)
+        hcopy(3)
+        smul(1, 1)
+        sturn(0, 2)
+        tanh(3, 1)
+        xturn(3, 1)
+        hdiff(1, 0, 2)
+        tanh(2, 1)
+        xturn(3, 0)
+        xcopy(3, 1, "S")
+        totals()
+        smul(0, 2)
+        sturn(3, 1)
+        tanh(1, 2)
+        zmul(4, 2)
+        hdiff(2, 0, 2)
+        zmul(2, 2)
+        xcopy(3, 0, "S")
+        sturn(2, 1)
+        tanh(4, 2)
+        sturn(1, 2)
+        smul(3, 1)
+        zmul(3, 2)
+        tanh(2, 2)
+        xquant(3)
+        gtotal(0)
+        gmix(1, "S")
+        smul(2, 1)
         smul(1, 2)
         zmul(1, 3)
-        hcopy(3)
-        sturn(3, 1)
-        hdiff(2, 0, 2)
-        gtotal()
-        tanh(0, 3)
-        tanh(1, 3)
-        smul(3, 1)
-        gmix(2, "S")
-        hdiff(0, 2, 4)
-        totals()
-        hdiff(1, 2, 4)
-        gmix(1, "S")
-        sturn(0, 3)
-        gquant(2)
-        zmul(2, 3)
-        smul(0, 3)
-        zmul(3, 3)
-        sturn(1, 3)
-        hjoin(0); alpha1(0); alpha2(0); alpha3(0)
-        squant(0)
-        tanh(3, 3)
-        aroot(0)
-        smul(1, 3)
-        tanh(2, 3)
-        zmul(4, 1)
-        sturn(3, 3)
-        gquant(1)
-        gt_rows_s()
-        zmul(3, 2)
-        smul(3, 3)
-        sturn(2, 3)
-        dmul(0)
+        zmul(0, 3)
         hdiff(3, 0, 2)
-        tanh(3, 2)
-        tanh(4, 1)
-        tanh(4, 2)
-        smul(2, 3)
-        zmul(4, 0)
-        sturn(4, 1)
-        tanh(4, 0)
-        ushift(0)
-        zmul(2, 2)
-        zmul(5, 0)
-        smul(4, 1)
-        tanh(2, 2)
-        zmul(4, 3)
-        gt_rows_v()
-        sturn(3, 2)
-        tanh(5, 0)
-        squant(1)
         sturn(2, 2)
-        usq(0)
-        hdiff(2, 2, 4)
-        zmul(5, 2)
-        dmul(1)
-        tanh(4, 3)
-        gfin(0)
-        tanh(5, 2)
-        smul(2, 2)
-        hcp(4, 1)
-        zmul(5, 3)
-        smul(3, 2)
-        sturn(5, 2)
-        tanh(5, 3)
-        squant(2)
-        sturn(4, 3)
-        sturn(4, 0)
-        squant(3)
-        zmul(6, 1)
-        smul(4, 3)
-        zmul(6, 3)
-        tanh(6, 1)
-        zmul(6, 0)
-        hjoin(2); alpha1(2); alpha2(2); alpha3(2)
-        dmul(2)
-        hcp(4, 3)
-        smul(4, 0)
-        aroot(2)
-        tanh(6, 3)
-        hjoin(1); alpha1(1); alpha2(1); alpha3(1)
-        smul(5, 2)
-        aroot(1)
-        hcp(4, 0)
         sturn(4, 2)
-        ushift(1)
-        zmul(5, 1)
-        hcp(5, 2)
-        sturn(5, 0)
+        gtotal(1)
+        smul(2, 2)
+        tanh(0, 3)
         smul(4, 2)
-        usq(1)
-        dmul(3)
-        ushift(2)
-        hcp(4, 2)
-        gfin(1)
-        squant(4)
-        usq(2)
-        sturn(5, 3)
+        tanh(1, 3)
+        zmul(3, 3)
+        hdiff(0, 2, 4)
+        gmix(3, "S")
+        sturn(0, 3)
+        zmul(6, 3)
+        gtotal(2)
+        smul(0, 3)
+        aroot(0, 2)
+        hdiff(1, 2, 4)
+        sturn(1, 3)
+        gtotal(3)
+        tanh(3, 2)
+        smul(1, 3)
+        aroot(1, 2)
+        gmix(2, "S")
+        squant(0)
+        zmul(2, 3)
+        sturn(3, 2)
+        squant(1)
+        gquant(3)
+        smul(3, 2)
+        tanh(2, 3)
+        gquant(1)
+        tanh(3, 3)
+        gquant(2)
+        zmul(5, 3)
+        tanh(6, 3)
+        sturn(2, 3)
+        hdiff(2, 2, 4)
+        dmul(1)
+        tanh(5, 3)
+        gt_rows_s()
         hdiff(3, 2, 4)
-        hmul(4)
+        aroot(2, 2)
+        sturn(3, 3)
+        zmul(4, 0)
+        zmul(5, 1)
+        smul(3, 3)
+        dmul(0)
+        tanh(4, 0)
+        aroot(3, 2)
+        smul(2, 3)
         tanh(5, 1)
-        gfin(2)
-        tanh(6, 0)
-        smul(5, 3)
-        hjoin(3); alpha1(3); alpha2(3); alpha3(3)
-        hcp(5, 3)
-        smul(5, 0)
-        aroot(3)
-        sturn(6, 0)
-        hout(4)
-        ushift(3)
+        squant(3)
+        sturn(4, 0)
+        squant(2)
         sturn(5, 1)
-        hcp(5, 0)
-        dmul(4)
-        smul(6, 0)
-        usq(3)
+        zmul(4, 3)
+        smul(4, 0)
+        zmul(4, 1)
         smul(5, 1)
-        gfin(3)
-        sturn(6, 1)
-        alpha1(4); alpha2(4); alpha3(4)
-        hcp(5, 1)
-        squant(5)
-        zmul(6, 2)
+        sturn(5, 3)
+        tanh(4, 3)
+        zmul(5, 2)
+        ushift(1)
+        tanh(4, 1)
         sturn(6, 3)
-        smul(6, 1)
-        tanh(6, 2)
-        aroot(4)
-        hmul(5)
-        smul(6, 3)
-        hdiff(6)
+        smul(5, 3)
+        sturn(4, 3)
+        tanh(5, 2)
+        dmul(2)
+        ushift(0)
+        usq(1)
+        smul(4, 3)
+        usq(0)
+        gt_rows_v()
+        dmul(3)
+        hdiff(4)
+        gfin(1)
         zmul(7, 3)
-        zmul(7, 1)
+        sturn(5, 2)
+        gfin(0)
         tanh(7, 3)
+        zmul(5, 0)
         zmul(7, 2)
-        hout(5)
-        ushift(4)
-        sturn(6, 2)
-        tanh(7, 1)
-        sturn(7, 3)
-        alpha1(6); alpha2(6); alpha3(6)
+        smul(5, 2)
+        sturn(4, 1)
+        tanh(5, 0)
+        ushift(2)
+        zmul(6, 0)
+        aroot(4, 1)
         tanh(7, 2)
-        smul(6, 2)
-        sturn(7, 1)
-        aroot(6)
-        usq(4)
-        zmul(7, 0)
-        alpha1(5); alpha2(5); alpha3(5)
-        smul(7, 1)
+        sturn(7, 3)
+        smul(4, 1)
+        zmul(6, 1)
+        usq(2)
+        smul(6, 3)
+        zmul(6, 2)
+        tanh(6, 0)
+        sturn(5, 0)
+        gfin(2)
+        squant(4)
+        tanh(6, 1)
         sturn(7, 2)
-        aroot(5)
-        tanh(7, 0)
-        dmul(5)
-        smul(7, 3)
-        gfin(4)
+        smul(5, 0)
+        zmul(7, 1)
+        tanh(6, 2)
+        dmul(4)
         smul(7, 2)
-        squant(6)
+        tanh(7, 1)
+        squant(5)
+        sturn(6, 2)
+        hdiff(5)
+        sturn(6, 0)
+        zmul(7, 0)
+        tanh(7, 0)
+        smul(6, 2)
+        aroot(5, 1)
+        smul(6, 0)
+        sturn(7, 1)
+        ushift(4)
+        sturn(6, 1)
+        smul(7, 1)
+        usq(4)
+        dmul(5)
+        smul(6, 1)
+        gfin(4)
+        ushift(3)
         sturn(7, 0)
-        smul(7, 0)
-        dmul(6)
+        squant(6)
+        usq(3)
         ushift(5)
-        squant(7)
+        dmul(6)
+        gfin(3)
+        smul(7, 0)
         usq(5)
-        ushift(6)
-        dmul(7, ((0, 256), (256, 512)))
+        hdiff(6)
         gfin(5)
-        hdiff(7)
+        smul(7, 3)
+        aroot(6, 1)
+        ushift(6)
+        squant(7)
         usq(6)
+        hdiff(7)
+        dmul(7, ((0, 256), (256, 512)))
         gfin(6)
-        alpha1(7); alpha2(7); alpha3(7)
         ushift(7, 256, 512)
+        aroot(7, 1)
         ushift(7, 0, 256)
         usq(7, 256, 512)
         usq(7, 0, 256)

@@ -56,13 +56,17 @@ def tile_obliquesoftsplitgaintable_d1p_kernel(tc, x_bytes, x_scale, p_words, p_s
         erow = kt([P, T], F32, "erow")
         gt2 = kt([P, T], F32, "gt2")
         warm = kt([P, 1], F32, "warm")
-        pows = kt([P, 2], F32, "pows")
+        pows = kt([P, 5], F32, "pows")
+        hds = kt([P, 8], F32, "hds")
+        hdp = kt([P, 4, 2], F32, "hdp")
+        al1 = kt([P, 8], F32, "al1")
+        al2 = kt([P, 8], F32, "al2")
+        al3 = kt([P, 1], F32, "al3")
         h_f = kt([P, 16], F32, "h_f")
-        root = [kt([P, 1], F32, "root%d" % i) for i in range(NM)]
+        roots = [kt([P, 8], F32, "root%d" % i) for i in range(NM)]
         junk = kt([P, 2048], BF16, "junk")
         swq = [kt([P, 512], U32, "swq%d" % i) for i in range(NM)]
         sws = [kt([P, 512], U8, "sws%d" % i) for i in range(NM)]
-        hd = [kt([P, 8], F32, "hd%d" % i) for i in range(NM)]
         st = {}
 
         xv = x_bytes.rearrange("(G r t) k -> G r (t k)", r=P, t=4)
@@ -86,11 +90,12 @@ def tile_obliquesoftsplitgaintable_d1p_kernel(tc, x_bytes, x_scale, p_words, p_s
             nc.sync.dma_start(out=xr[G][:], in_=xv[G])
         for G in range(NG):
             nc.sync.dma_start(out=graw[G][:], in_=gv[G])
-        make_identity(nc, ident_f[:])
         make_identity(nc, ident_b[:])
+        make_identity(nc, ident_f[:])
         nc.gpsimd.memset(warm[:], 0.0)
-        nc.gpsimd.memset(pows[:, 0:1], -0.5)
-        nc.gpsimd.memset(pows[:, 1:2], -1.0)
+        nc.gpsimd.memset(hdp[:], 0.0)
+        nc.gpsimd.memset(pows[:, 0:4], -0.5)
+        nc.gpsimd.memset(pows[:, 4:5], -1.0)
         S.activation(out=warm[:], in_=warm[:], func=ACT.Tanh)
 
         def xprod(G, t, eng, js=(0, 1, 2, 3)):
@@ -132,6 +137,8 @@ def tile_obliquesoftsplitgaintable_d1p_kernel(tc, x_bytes, x_scale, p_words, p_s
             st["gg", G] = gg
             if eng == "V":
                 V.tensor_copy(out=gg[:], in_=graw[G][:].rearrange("p t n -> p n t"))
+            elif eng == "G":
+                nc.gpsimd.tensor_scalar(out=gg[:], in0=graw[G][:].rearrange("p t n -> p n t"), scalar1=1.0, scalar2=0.0, op0=ALU.mult, op1=ALU.add)
             else:
                 S.copy(out=gg[:], in_=graw[G][:].rearrange("p t n -> p n t"))
 
@@ -163,23 +170,30 @@ def tile_obliquesoftsplitgaintable_d1p_kernel(tc, x_bytes, x_scale, p_words, p_s
                             in1=wh[:, G:G + 1, :].to_broadcast([P, P, 4]), op=ALU.mult)
 
         def hdiff(m, G0=0, G1=NG):
-            o = hd[m][:, 0:1] if G1 - G0 == NG else hd[m][:, 4 + G0 // 2:5 + G0 // 2]
+            o = hds[:, m:m + 1] if G1 - G0 == NG else hdp[:, m, G0 // 2:G0 // 2 + 1]
             V.scalar_tensor_tensor(out=junk[:, 512 * G0:512 * G1], in0=st["s", m][:, 512 * G0:512 * G1], scalar=1.0, in1=h_all[:, 512 * G0:512 * G1],
                                    op0=ALU.mult, op1=ALU.mult, accum_out=o)
-
-        def hjoin(m):
-            V.tensor_tensor(out=hd[m][:, 0:1], in0=hd[m][:, 4:5], in1=hd[m][:, 5:6], op=ALU.add)
 
         def squant(m):
             V.quantize_mx(out=swq[m][:].bitcast(FP8X4), scales=sws[m][:], in_=st["sw", m][:])
 
-        def aroot(m, pieces):
-            GP = nc.gpsimd
-            if pieces == 2:
-                GP.tensor_tensor(out=hd[m][:, 0:1], in0=hd[m][:, 4:5], in1=hd[m][:, 5:6], op=ALU.add)
-            GP.tensor_scalar(out=hd[m][:, 1:2], in0=hd[m][:, 0:1], scalar1=sc[:, 3:4], scalar2=2.0, op0=ALU.mult, op1=ALU.add)
-            GP.tensor_scalar(out=hd[m][:, 2:3], in0=hd[m][:, 0:1], scalar1=sc[:, 1:2], scalar2=hd[m][:, 1:2], op0=ALU.add, op1=ALU.mult)
-            GP.tensor_tensor(out=root[m][:], in0=hd[m][:, 2:3], in1=pows[:, 0:1], op=ALU.pow)
+        def hjoin(i):
+            V.tensor_reduce(out=hds[:, 0:4], in_=hdp[:], axis=AX.X, op=ALU.add)
+
+        def alpha_a(m0, m1):
+            V.tensor_scalar(out=al1[:, m0:m1], in0=hds[:, m0:m1], scalar1=sc[:, 3:4], scalar2=2.0, op0=ALU.mult, op1=ALU.add)
+
+        def alpha_b(m0, m1):
+            V.scalar_tensor_tensor(out=al2[:, m0:m1], in0=hds[:, m0:m1], scalar=sc[:, 1:2], in1=al1[:, m0:m1], op0=ALU.add, op1=ALU.mult)
+
+        def aroot(m0, m1):
+            r = roots[m0]
+            nc.gpsimd.tensor_tensor(out=r[:, 0:m1 - m0], in0=al2[:, m0:m1], in1=pows[:, 0:m1 - m0], op=ALU.pow)
+            for m in range(m0, m1):
+                st["root", m] = r[:, m - m0:m - m0 + 1]
+
+        def arecip(m0, m1):
+            V.reciprocal(out=al3[:], in_=al2[:, m0:m1])
 
         def dmul(m, cols=((0, T),)):
             d = psum.tile([P, T], F32, name="d", tag="d", bufs=2)
@@ -195,10 +209,15 @@ def tile_obliquesoftsplitgaintable_d1p_kernel(tc, x_bytes, x_scale, p_words, p_s
             return st[kind, m]
 
         def ushift(m, c0=0, c1=T):
-            V.scalar_tensor_tensor(out=tile3("u", m)[:, c0:c1], in0=gtn[:, c0:c1], scalar=hd[m][:, 0:1], in1=st["d", m][:, c0:c1], op0=ALU.mult, op1=ALU.add)
+            V.scalar_tensor_tensor(out=tile3("u", m)[:, c0:c1], in0=gtn[:, c0:c1], scalar=hds[:, m:m + 1], in1=st["d", m][:, c0:c1], op0=ALU.mult, op1=ALU.add)
 
         def usq(m, c0=0, c1=T):
-            S.activation(out=tile3("q", m)[:, c0:c1], in_=st["u", m][:, c0:c1], func=ACT.Square, scale=root[m][:])
+            S.activation(out=tile3("q", m)[:, c0:c1], in_=st["u", m][:, c0:c1], func=ACT.Square, scale=st["root", m] if m < NM - 1 else 1.0)
+
+        def vfin(m):
+            o = tile3("o", m)
+            V.tensor_tensor(out=o[:], in0=st["q", m][:], in1=erow[:], op=ALU.subtract)
+            nc.sync.dma_start(out=out[P * m:P * (m + 1), :], in_=o[:])
 
         def gfin(m):
             o = tile3("o", m)
@@ -208,25 +227,31 @@ def tile_obliquesoftsplitgaintable_d1p_kernel(tc, x_bytes, x_scale, p_words, p_s
         def hcp(m, G):
             if ("sT", m) not in st:
                 st["sT", m] = work.tile([P, 2048], F32, name="sT", bufs=2, align_bytes=64)
-            S.copy(out=st["sT", m][:, 512 * G:512 * (G + 1)], in_=st["tr", m, G][:].rearrange("p t m -> p (t m)"))
+            for t in range(4):
+                S.activation(out=st["sT", m][:, 512 * G + P * t:512 * G + P * (t + 1)], in_=st["tr", m, G][:, t, :], func=ACT.Copy, scale=h_f[:, 4 * G + t:4 * G + t + 1])
 
         def hmul(m):
-            ha = psum.tile([P, 2], F32, name="ha", tag="d", bufs=2)
+            ha = psum.tile([P, P], F32, name="ha", tag="d", bufs=2)
             st["ha", m] = ha
             for i in range(16):
-                PE.matmul(ha[:, 0:1], lhsT=st["sT", m][:, P * i:P * (i + 1)], rhs=h_f[:, i:i + 1], start=(i == 0), stop=(i == 15))
+                PE.matmul(ha[:], lhsT=st["sT", m][:, P * i:P * (i + 1)], rhs=ident_f[:], start=(i == 0), stop=(i == 15), is_transpose=True)
 
         def hout(m):
             ha = st["ha", m]
-            V.tensor_copy(out=hd[m][:, 0:1], in_=ha[:, 0:1])
+            V.tensor_reduce(out=hdp[:, m, 0:1] if m < 4 else hds[:, m:m + 1], in_=ha[:], axis=AX.X, op=ALU.add)
 
         def fin(m, c0=0, c1=T):
             o = tile3("o", m)
-            V.tensor_tensor(out=o[:, c0:c1], in0=st["q", m][:, c0:c1], in1=erow[:, c0:c1], op=ALU.subtract)
+            V.scalar_tensor_tensor(out=o[:, c0:c1], in0=st["q", m][:, c0:c1], scalar=al3[:], in1=erow[:, c0:c1], op0=ALU.mult, op1=ALU.subtract)
             nc.sync.dma_start(out=out[P * m:P * (m + 1), c0:c1], in_=o[:, c0:c1])
 
+        def warm_up():
+            if "wm" not in st:
+                st["wm"] = psum.tile([P, 4, P], F32, name="wm", tag="d", bufs=2)
+            PE.matmul(st["wm"][:], lhsT=ident_b[:], rhs=ident_b[:].unsqueeze(1).to_broadcast([P, 4, P]), start=True, stop=True)
+
         def turn_rows():
-            t_ps = psum.tile([P, 5, P], BF16, name="rt", tag="d", bufs=2)
+            t_ps = psum.tile([P, 5, P], BF16, name="rt", tag="tr", bufs=3)
             for t in range(4):
                 PE.transpose(t_ps[:, t, :], rows[:, t:512:4], ident_b[:])
             PE.transpose(t_ps[:, 4, :], rows[:, 512:640], ident_b[:])
@@ -239,7 +264,7 @@ def tile_obliquesoftsplitgaintable_d1p_kernel(tc, x_bytes, x_scale, p_words, p_s
             V.tensor_scalar(out=hb[:], in0=t_ps[:, 4, 0:8], scalar1=0.5, scalar2=None, op0=ALU.mult)
 
         def hspread(G):
-            t_ps = psum.tile([P, 512], F32, name="hs", tag="d", bufs=2)
+            t_ps = psum.tile([P, 512], F32, name="hs", tag="tr" if G < 2 else "d", bufs=3 if G < 2 else 2)
             st["hs", G] = t_ps
             for t in range(4):
                 PE.matmul(t_ps[:, P * t:P * (t + 1)], lhsT=wh[:, 4 + G, t:t + 1].to_broadcast([P, P]), rhs=ident_b[:], start=True, stop=True)
@@ -257,11 +282,11 @@ def tile_obliquesoftsplitgaintable_d1p_kernel(tc, x_bytes, x_scale, p_words, p_s
             GP = nc.gpsimd
             V.tensor_reduce(out=sc[:, 0:1], in_=ht4[:], axis=AX.X, op=ALU.add)
             GP.tensor_scalar(out=sc[:, 1:2], in0=sc[:, 0:1], scalar1=1.0, scalar2=2.0 * LAM, op0=ALU.mult, op1=ALU.add)
-            GP.tensor_tensor(out=sc[:, 2:3], in0=sc[:, 1:2], in1=pows[:, 1:2], op=ALU.pow)
+            GP.tensor_tensor(out=sc[:, 2:3], in0=sc[:, 1:2], in1=pows[:, 4:5], op=ALU.pow)
             GP.tensor_scalar(out=sc[:, 3:4], in0=sc[:, 2:3], scalar1=-2.0, scalar2=0.0, op0=ALU.mult, op1=ALU.add)
             GP.tensor_scalar(out=sc[:, 4:5], in0=sc[:, 2:3], scalar1=-1.0, scalar2=0.0, op0=ALU.mult, op1=ALU.add)
             GP.tensor_scalar(out=sc[:, 5:6], in0=sc[:, 0:1], scalar1=LAM, scalar2=sc[:, 1:2], op0=ALU.add, op1=ALU.mult)
-            GP.tensor_tensor(out=sc[:, 6:7], in0=sc[:, 5:6], in1=pows[:, 1:2], op=ALU.pow)
+            GP.tensor_tensor(out=sc[:, 6:7], in0=sc[:, 5:6], in1=pows[:, 4:5], op=ALU.pow)
             GP.tensor_scalar(out=sc[:, 7:8], in0=sc[:, 6:7], scalar1=0.5 * LAM, scalar2=0.0, op0=ALU.mult, op1=ALU.add)
 
         def gt_rows_s():
@@ -271,256 +296,280 @@ def tile_obliquesoftsplitgaintable_d1p_kernel(tc, x_bytes, x_scale, p_words, p_s
         def gt_rows_v():
             V.tensor_scalar(out=erow[:], in0=gt2[:], scalar1=sc[:, 7:8], scalar2=None, op0=ALU.mult)
 
-        xprod(0, 0, "V")
         xprod(0, 3, "S")
+        xprod(0, 0, "V")
         xprod(0, 2, "V")
-        turn_rows()
         xprod(0, 1, "V")
-        xprod(1, 3, "V")
-        xturn(0, 1)
-        xprod(1, 1, "V")
-        rows_out()
         xprod(1, 2, "V")
+        xprod(1, 1, "S")
+        warm_up()
+        warm_up()
+        warm_up()
+        warm_up()
+        warm_up()
+        turn_rows()
+        xturn(0, 1)
         xturn(0, 0)
-        xprod(2, 3, "V")
         xcopy(0, 1, "S")
-        xprod(2, 0, "V")
+        rows_out()
+        hspread(1)
+        xprod(2, 3, "V")
         xprod(1, 0, "V")
-        xturn(1, 1)
-        xcopy(0, 0, "S")
         xquant(0, 256, 512)
-        xprod(3, 1, "V")
-        gmix(0, "S")
-        xprod(2, 2, "V")
-        xturn(1, 0)
+        xprod(3, 0, "V")
+        xcopy(0, 0, "S")
+        xprod(1, 3, "V")
         xquant(0, 0, 256)
         xprod(2, 1, "V")
-        zmul(2, 0)
-        xprod(3, 3, "V")
-        zmul(1, 0)
-        xprod(3, 2, "V")
-        zmul(3, 0)
-        xprod(3, 0, "V")
-        xcopy(1, 0, "S")
-        gquant(0)
-        tanh(3, 0)
-        xturn(2, 0)
-        xcopy(1, 1, "S")
-        sturn(3, 0)
-        tanh(2, 0)
-        xquant(1)
-        zmul(0, 0)
-        xcopy(2, 0, "S")
-        xturn(2, 1)
-        smul(3, 0)
-        tanh(0, 0)
-        sturn(2, 0)
-        zmul(0, 1)
-        xcopy(2, 1, "S")
-        sturn(0, 0)
-        smul(2, 0)
-        tanh(1, 0)
-        hspread(1)
-        xquant(2)
-        zmul(1, 1)
-        tanh(0, 1)
+        xprod(3, 2, "S")
         hspread(0)
-        smul(0, 0)
-        sturn(1, 0)
-        hcopy(1)
-        sturn(0, 1)
+        xprod(2, 2, "S")
+        xturn(1, 0)
+        xturn(1, 1)
+        xcopy(1, 0, "S")
+        gmix(0, "V")
+        xcopy(1, 1, "S")
+        zmul(0, 0)
+        zmul(1, 0)
+        xquant(1)
+        tanh(0, 0)
+        xprod(2, 0, "V")
+        xturn(2, 1)
+        xprod(3, 1, "V")
+        zmul(2, 0)
+        zmul(3, 0)
+        tanh(1, 0)
+        sturn(0, 0)
+        xcopy(2, 1, "V")
+        tanh(2, 0)
         hcopy(0)
+        xturn(2, 0)
+        xcopy(2, 0, "V")
+        hcopy(1)
+        zmul(0, 1)
+        zmul(1, 1)
+        tanh(3, 0)
+        sturn(1, 0)
+        sturn(2, 0)
+        smul(0, 0)
+        tanh(0, 1)
         smul(1, 0)
-        zmul(0, 2)
+        xprod(3, 3, "S")
+        xturn(3, 0)
+        zmul(2, 1)
         zmul(3, 1)
         tanh(1, 1)
-        smul(0, 1)
-        hspread(2)
-        hspread(3)
-        tanh(0, 2)
-        hdiff(0, 0, 2)
-        sturn(1, 1)
-        hcopy(2)
-        zmul(2, 1)
-        zmul(1, 2)
-        hcopy(3)
-        smul(1, 1)
-        sturn(0, 2)
-        tanh(3, 1)
-        xturn(3, 1)
-        hdiff(1, 0, 2)
+        sturn(3, 0)
+        sturn(0, 1)
+        smul(2, 0)
+        hcp(2, 0)
+        xquant(2)
+        gquant(0)
         tanh(2, 1)
-        xturn(3, 0)
-        xcopy(3, 1, "S")
-        totals()
-        smul(0, 2)
-        sturn(3, 1)
-        tanh(1, 2)
-        zmul(4, 2)
-        hdiff(2, 0, 2)
-        zmul(2, 2)
-        xcopy(3, 0, "S")
+        smul(3, 0)
+        xturn(3, 1)
+        gmix(1, "G")
+        zmul(0, 2)
+        zmul(1, 2)
+        tanh(3, 1)
+        sturn(1, 1)
         sturn(2, 1)
-        tanh(4, 2)
-        sturn(1, 2)
-        smul(3, 1)
-        zmul(3, 2)
-        tanh(2, 2)
+        smul(0, 1)
+        xcopy(3, 0, "S")
+        hdiff(0, 0, 2)
+        xcopy(3, 1, "S")
+        tanh(0, 2)
+        smul(1, 1)
         xquant(3)
-        gtotal(0)
-        gmix(1, "S")
+        hspread(2)
+        hcopy(2)
+        zmul(2, 2)
+        zmul(3, 2)
+        tanh(1, 2)
+        sturn(3, 1)
+        sturn(0, 2)
         smul(2, 1)
-        smul(1, 2)
-        zmul(1, 3)
-        zmul(0, 3)
-        hdiff(3, 0, 2)
-        sturn(2, 2)
-        sturn(4, 2)
-        gtotal(1)
-        smul(2, 2)
-        tanh(0, 3)
-        smul(4, 2)
-        tanh(1, 3)
-        zmul(3, 3)
-        hdiff(0, 2, 4)
-        gmix(3, "S")
-        sturn(0, 3)
-        zmul(6, 3)
-        gtotal(2)
-        smul(0, 3)
-        aroot(0, 2)
-        hdiff(1, 2, 4)
-        sturn(1, 3)
-        gtotal(3)
-        tanh(3, 2)
-        smul(1, 3)
-        aroot(1, 2)
-        gmix(2, "S")
-        squant(0)
-        zmul(2, 3)
-        sturn(3, 2)
-        squant(1)
-        gquant(3)
-        smul(3, 2)
-        tanh(2, 3)
+        hcp(2, 1)
+        hspread(3)
         gquant(1)
-        tanh(3, 3)
-        gquant(2)
-        zmul(5, 3)
-        tanh(6, 3)
-        sturn(2, 3)
-        hdiff(2, 2, 4)
-        dmul(1)
-        tanh(5, 3)
-        gt_rows_s()
-        hdiff(3, 2, 4)
-        aroot(2, 2)
-        sturn(3, 3)
+        tanh(2, 2)
+        smul(3, 1)
+        hdiff(1, 0, 2)
+        zmul(0, 3)
+        zmul(1, 3)
+        tanh(3, 2)
+        sturn(1, 2)
+        sturn(2, 2)
+        smul(0, 2)
+        tanh(0, 3)
+        smul(1, 2)
+        hcopy(3)
+        zmul(2, 3)
+        zmul(3, 3)
+        tanh(1, 3)
+        sturn(3, 2)
+        sturn(0, 3)
+        smul(2, 2)
+        hcp(2, 2)
+        gtotal(0)
+        tanh(2, 3)
+        smul(3, 2)
+        gtotal(1)
+        gmix(3, "S")
         zmul(4, 0)
-        zmul(5, 1)
-        smul(3, 3)
-        dmul(0)
-        tanh(4, 0)
-        aroot(3, 2)
-        smul(2, 3)
-        tanh(5, 1)
-        squant(3)
-        sturn(4, 0)
-        squant(2)
-        sturn(5, 1)
-        zmul(4, 3)
-        smul(4, 0)
         zmul(4, 1)
-        smul(5, 1)
-        sturn(5, 3)
-        tanh(4, 3)
-        zmul(5, 2)
-        ushift(1)
+        tanh(3, 3)
+        sturn(1, 3)
+        sturn(2, 3)
+        smul(0, 3)
+        gtotal(2)
+        hdiff(0, 2, 4)
+        squant(0)
+        hdiff(1, 2, 4)
+        tanh(4, 0)
+        smul(1, 3)
+        gquant(3)
+        gmix(2, "G")
+        zmul(4, 2)
+        zmul(4, 3)
         tanh(4, 1)
-        sturn(6, 3)
-        smul(5, 3)
-        sturn(4, 3)
-        tanh(5, 2)
-        dmul(2)
-        ushift(0)
-        usq(1)
-        smul(4, 3)
-        usq(0)
-        gt_rows_v()
-        dmul(3)
-        hdiff(4)
-        gfin(1)
-        zmul(7, 3)
-        sturn(5, 2)
-        gfin(0)
-        tanh(7, 3)
+        sturn(3, 3)
+        sturn(4, 0)
+        smul(2, 3)
+        hcp(2, 3)
+        hdiff(3, 2, 4)
+        totals()
+        gtotal(3)
+        hdiff(3, 0, 2)
+        tanh(4, 2)
+        smul(3, 3)
+        gt_rows_s()
+        hmul(2)
         zmul(5, 0)
-        zmul(7, 2)
-        smul(5, 2)
+        zmul(5, 1)
+        tanh(4, 3)
         sturn(4, 1)
+        sturn(4, 2)
+        smul(4, 0)
+        hcp(4, 0)
+        squant(1)
+        gquant(2)
         tanh(5, 0)
-        ushift(2)
-        zmul(6, 0)
-        aroot(4, 1)
-        tanh(7, 2)
-        sturn(7, 3)
         smul(4, 1)
-        zmul(6, 1)
-        usq(2)
-        smul(6, 3)
-        zmul(6, 2)
-        tanh(6, 0)
+        hcp(4, 1)
+        hout(2)
+        dmul(0)
+        squant(3)
+        hjoin(0)
+        gt_rows_v()
+        zmul(5, 2)
+        zmul(5, 3)
+        tanh(5, 1)
+        sturn(4, 3)
         sturn(5, 0)
-        gfin(2)
-        squant(4)
-        tanh(6, 1)
-        sturn(7, 2)
+        smul(4, 2)
+        hcp(4, 2)
+        ushift(0)
+        dmul(1)
+        alpha_a(0, 4)
+        tanh(5, 2)
+        smul(4, 3)
+        hcp(4, 3)
+        alpha_b(0, 4)
+        squant(2)
+        zmul(6, 0)
+        zmul(6, 1)
+        tanh(5, 3)
+        sturn(5, 1)
+        sturn(5, 2)
         smul(5, 0)
-        zmul(7, 1)
-        tanh(6, 2)
-        dmul(4)
-        smul(7, 2)
-        tanh(7, 1)
-        squant(5)
-        sturn(6, 2)
-        hdiff(5)
+        hmul(4)
+        aroot(0, 4)
+        ushift(1)
+        usq(0)
+        tanh(6, 0)
+        smul(5, 1)
+        squant(4)
+        zmul(6, 2)
+        zmul(6, 3)
+        tanh(6, 1)
+        sturn(5, 3)
         sturn(6, 0)
+        smul(5, 2)
+        hout(4)
+        hdiff(5)
+        gfin(0)
+        dmul(2)
+        tanh(6, 2)
+        smul(5, 3)
+        dmul(3)
+        usq(1)
+        gfin(1)
         zmul(7, 0)
-        tanh(7, 0)
-        smul(6, 2)
-        aroot(5, 1)
-        smul(6, 0)
-        sturn(7, 1)
-        ushift(4)
+        zmul(7, 1)
+        tanh(6, 3)
         sturn(6, 1)
-        smul(7, 1)
-        usq(4)
-        dmul(5)
-        smul(6, 1)
-        gfin(4)
+        sturn(6, 2)
+        smul(6, 0)
+        hcp(6, 0)
+        ushift(2)
         ushift(3)
-        sturn(7, 0)
-        squant(6)
+        dmul(4)
+        usq(2)
         usq(3)
-        ushift(5)
-        dmul(6)
+        tanh(7, 0)
+        smul(6, 1)
+        hcp(6, 1)
+        alpha_a(4, 6)
+        squant(5)
+        vfin(2)
         gfin(3)
+        zmul(7, 2)
+        zmul(7, 3)
+        tanh(7, 1)
+        sturn(6, 3)
+        sturn(7, 0)
+        smul(6, 2)
+        hcp(6, 2)
+        alpha_b(4, 6)
+        dmul(5)
+        aroot(4, 6)
+        ushift(4)
+        tanh(7, 2)
+        smul(6, 3)
+        hcp(6, 3)
+        squant(6)
+        ushift(5)
+        hmul(6)
+        usq(4)
+        tanh(7, 3)
+        sturn(7, 1)
+        sturn(7, 2)
         smul(7, 0)
-        usq(5)
-        hdiff(6)
-        gfin(5)
+        hout(6)
+        smul(7, 1)
+        sturn(7, 3)
+        smul(7, 2)
         smul(7, 3)
-        aroot(6, 1)
-        ushift(6)
+        alpha_a(6, 7)
         squant(7)
-        usq(6)
         hdiff(7)
+        dmul(6)
         dmul(7, ((0, 256), (256, 512)))
-        gfin(6)
-        ushift(7, 256, 512)
-        aroot(7, 1)
+        alpha_b(6, 7)
+        usq(5)
+        alpha_a(7, 8)
         ushift(7, 0, 256)
-        usq(7, 256, 512)
+        gfin(4)
         usq(7, 0, 256)
-        fin(7, 256, 512)
+        ushift(6)
+        alpha_b(7, 8)
+        ushift(7, 256, 512)
+        arecip(7, 8)
+        gfin(5)
+        aroot(6, 7)
+        usq(6)
         fin(7, 0, 256)
+        vfin(6)
+        usq(7, 256, 512)
+        fin(7, 256, 512)

@@ -5,9 +5,16 @@ from concourse.masks import make_identity
 
 N, D, M, T = 2048, 512, 1024, 512
 P = 128
-NG = N // 512
+GROUP = 512
+NG = N // GROUP
 NM = M // P
+TILES = GROUP // P
+SCALES = D // P
+HALF_GROUP = GROUP // 2
+LAST = NM - 1
 LAM = 64.0
+BY_GROUP = 4
+TURNED = (2, 4, 6)
 FLOPS = 2 * N * D * M + 2 * N * M * T + 2 * N * T + 2 * N * M
 
 F32 = mybir.dt.float32
@@ -25,551 +32,395 @@ AX = mybir.AxisListType
 
 def tile_obliquesoftsplitgaintable_d1p_kernel(tc, x_bytes, x_scale, p_words, p_scales, b, w, g, h, out):
     nc = tc.nc
-    V, S, PE = nc.vector, nc.scalar, nc.tensor
+    V, S, PE, GP = nc.vector, nc.scalar, nc.tensor, nc.gpsimd
     with ExitStack() as ctx:
-        keep = ctx.enter_context(tc.tile_pool(name="keep", bufs=1))
+        keep_pool = ctx.enter_context(tc.tile_pool(name="keep", bufs=1))
         work = ctx.enter_context(tc.tile_pool(name="work", bufs=2))
         psum = ctx.enter_context(tc.psum_pool(name="psum", bufs=2))
         ctx.enter_context(tc.manual_schedule())
 
-        def kt(shape, dt, name):
-            return keep.tile(shape, dt, name=name, align_bytes=64)
+        def keep(shape, dtype, name):
+            return keep_pool.tile(shape, dtype, name=name, align_bytes=64)
 
-        ident_f = kt([P, P], F32, "ident_f")
-        ident_b = kt([P, P], BF16, "ident_b")
-        xs = kt([P, NG, 16], F32, "xs")
-        xr = [kt([P, 2048], U8, "xr%d" % i) for i in range(NG)]
-        xq = kt([P, NG, 512], U32, "xq")
-        xqs = kt([P, NG, 512], U8, "xqs")
-        pw = kt([P, 2048], U8, "pw")
-        psc = kt([P, M], U8, "psc")
-        rows = kt([P, 640], BF16, "rows")
-        wh = kt([P, 8, 4], BF16, "wh")
-        hb = kt([P, 8], F32, "hb")
-        h_all = kt([P, 2048], BF16, "h_all")
-        ht4 = kt([P, 4], F32, "ht4")
-        sc = kt([P, 8], F32, "sc")
-        graw = [kt([P, 4, T], BF16, "graw%d" % i) for i in range(NG)]
-        gq = kt([P, NG, T], U32, "gq")
-        gqs = kt([P, NG, T], U8, "gqs")
-        gtn = kt([P, T], F32, "gtn")
-        erow = kt([P, T], F32, "erow")
-        gt2 = kt([P, T], F32, "gt2")
-        warm = kt([P, 1], F32, "warm")
-        pows = kt([P, 5], F32, "pows")
-        hds = kt([P, 8], F32, "hds")
-        hdp = kt([P, 4, 2], F32, "hdp")
-        al1 = kt([P, 8], F32, "al1")
-        al2 = kt([P, 8], F32, "al2")
-        al3 = kt([P, 1], F32, "al3")
-        h_f = kt([P, 16], F32, "h_f")
-        roots = [kt([P, 8], F32, "root%d" % i) for i in range(NM)]
-        junk = kt([P, 2048], BF16, "junk")
-        swq = [kt([P, 512], U32, "swq%d" % i) for i in range(NM)]
-        sws = [kt([P, 512], U8, "sws%d" % i) for i in range(NM)]
-        st = {}
+        def z_bank():
+            return psum.tile([P, GROUP], F32, name="z", tag="z", bufs=3)
 
-        xv = x_bytes.rearrange("(G r t) k -> G r (t k)", r=P, t=4)
-        gv = g.rearrange("(G p t) n -> G p t n", p=P, t=4)
-        xsv = x_scale.rearrange("(G r t) j -> G r (t j)", r=P, t=4)
-        nc.scalar.dma_start(out=xs[:, 0, :], in_=xsv[0])
-        for t in range(4):
-            nc.sync.dma_start(out=xr[0][:, 512 * t:512 * (t + 1)], in_=xv[0][:, 512 * t:512 * (t + 1)])
+        def turn_bank(shape, dtype, name):
+            return psum.tile(shape, dtype, name=name, tag="turn", bufs=3)
+
+        def other_bank(shape, name):
+            return psum.tile(shape, F32, name=name, tag="other", bufs=2)
+
+        ident_f = keep([P, P], F32, "ident_f")
+        ident_b = keep([P, P], BF16, "ident_b")
+        x_raw = [keep([P, TILES * D], U8, "x_raw%d" % grp) for grp in range(NG)]
+        x_sc = keep([P, NG, TILES * SCALES], F32, "x_sc")
+        x_q = keep([P, NG, GROUP], U32, "x_q")
+        x_q_sc = keep([P, NG, GROUP], U8, "x_q_sc")
+        p_q = keep([P, 2 * M], U8, "p_q")
+        p_q_sc = keep([P, M], U8, "p_q_sc")
+        rows = keep([P, GROUP + P], BF16, "rows")
+        wh = keep([P, 2 * NG, TILES], BF16, "wh")
+        h_col = keep([P, NG * TILES], F32, "h_col")
+        b_half = keep([P, NM], F32, "b_half")
+        h_row = keep([P, N], BF16, "h_row")
+        ht_part = keep([P, NG], F32, "ht_part")
+        ht, s_sum, s_inv, s_m2inv, s_m1inv, e_den, e_inv, e_fac = [keep([P, 1], F32, "total%d" % i) for i in range(8)]
+        g_raw = [keep([P, TILES, T], BF16, "g_raw%d" % grp) for grp in range(NG)]
+        g_q = keep([P, NG, T], U32, "g_q")
+        g_q_sc = keep([P, NG, T], U8, "g_q_sc")
+        gt_shift = keep([P, T], F32, "gt_shift")
+        gt_sq = keep([P, T], F32, "gt_sq")
+        last_term = keep([P, T], F32, "last_term")
+        hd_part = keep([P, BY_GROUP, 2], F32, "hd_part")
+        hd = keep([P, NM], F32, "hd")
+        den_a = keep([P, NM], F32, "den_a")
+        den = keep([P, NM], F32, "den")
+        den_root = {mt: keep([P, BY_GROUP], F32, "den_root%d" % mt) for mt in (0, 4, 6)}
+        den_inv = keep([P, 1], F32, "den_inv")
+        exponents = keep([P, BY_GROUP + 1], F32, "exponents")
+        first_tanh = keep([P, 1], F32, "first_tanh")
+        product = keep([P, N], BF16, "product")
+        sw_q = [keep([P, NG * P], U32, "sw_q%d" % mt) for mt in range(NM)]
+        sw_q_sc = [keep([P, NG * P], U8, "sw_q_sc%d" % mt) for mt in range(NM)]
+        live = {}
+
+        def handed(key, make):
+            if key not in live:
+                live[key] = make()
+            return live[key]
+
+        x_view = x_bytes.rearrange("(grp r j) k -> grp r (j k)", r=P, j=TILES)
+        g_view = g.rearrange("(grp r j) t -> grp r j t", r=P, j=TILES)
         V.memset(rows[:], 0.0)
-        V.memset(psc[:].bitcast(I32), 0)
-        nc.scalar.dma_start(out=rows[0:4, 0:512], in_=w.rearrange("(G f) -> G f", G=4))
-        nc.scalar.dma_start(out=rows[4:8, 0:512], in_=h.rearrange("(G f) -> G f", G=4))
-        nc.scalar.dma_start(out=rows[0:8, 512:640], in_=b.rearrange("(c p) -> c p", p=P))
-        for G in range(1, NG):
-            nc.scalar.dma_start(out=xs[:, G, :], in_=xsv[G])
-        for q in range(4):
-            nc.scalar.dma_start(out=psc[32 * q:32 * q + 4, :].bitcast(I32), in_=p_scales[0, 4 * q:4 * q + 4, :].bitcast(I32))
-        nc.sync.dma_start(out=xr[1][:], in_=xv[1])
-        nc.sync.dma_start(out=pw[:].bitcast(I32), in_=p_words[0].bitcast(I32))
-        for G in range(2, NG):
-            nc.sync.dma_start(out=xr[G][:], in_=xv[G])
-        for G in range(NG):
-            nc.sync.dma_start(out=graw[G][:], in_=gv[G])
+        V.memset(p_q_sc[:].bitcast(I32), 0)
+        GP.memset(first_tanh[:], 0.0)
         make_identity(nc, ident_b[:])
         make_identity(nc, ident_f[:])
-        nc.gpsimd.memset(warm[:], 0.0)
-        nc.gpsimd.memset(hdp[:], 0.0)
-        nc.gpsimd.memset(pows[:, 0:4], -0.5)
-        nc.gpsimd.memset(pows[:, 4:5], -1.0)
-        S.activation(out=warm[:], in_=warm[:], func=ACT.Tanh)
-
-        def xprod(G, t, eng, js=(0, 1, 2, 3)):
-            if ("xb", G) not in st:
-                st["xb", G] = work.tile([P, 4, 512], BF16, name="xb", bufs=4, align_bytes=64)
-            xb = st["xb", G]
-            for j in js:
-                o = xb[:, t, 128 * j:128 * (j + 1)]
-                i = xr[G][:, 512 * t + 128 * j:512 * t + 128 * (j + 1)].bitcast(FP8)
-                s1 = xs[:, G, 4 * t + j:4 * t + j + 1]
-                if eng == "V":
-                    V.tensor_scalar(out=o, in0=i, scalar1=s1, scalar2=None, op0=ALU.mult)
-                else:
-                    S.activation(out=o, in_=i, func=ACT.Copy, scale=s1)
-
-        def xturn(G, a):
-            t_ps = psum.tile([P, 2, 2, P], F32, name="turn", tag="d", bufs=2)
-            st["xt", G, a] = t_ps
-            for i in range(2):
-                words = st["xb", G][:, 2 * a + i, :].bitcast(F32)
-                for u in range(2):
-                    PE.transpose(t_ps[:, i, u, :], words[:, u:256:2], ident_f[:])
-
-        def xcopy(G, a, eng):
-            if ("gx", G) not in st:
-                st["gx", G] = work.tile([P, 2048], BF16, name="gx", bufs=3, align_bytes=64)
-            o = st["gx", G][:, 1024 * a:1024 * (a + 1)].bitcast(F32).rearrange("p (i r u) -> p i r u", i=2, u=2)
-            i = st["xt", G, a][:].rearrange("p i u r -> p i r u")
-            if eng == "V":
-                V.tensor_copy(out=o, in_=i)
-            else:
-                S.copy(out=o, in_=i)
-
-        def xquant(G, c0=0, c1=512):
-            V.quantize_mx(out=xq[:, G, c0:c1].bitcast(FP8X4), scales=xqs[:, G, c0:c1], in_=st["gx", G][:, 4 * c0:4 * c1])
-
-        def gmix(G, eng):
-            gg = work.tile([P, T, 4], BF16, name="gg", bufs=3, align_bytes=64)
-            st["gg", G] = gg
-            if eng == "V":
-                V.tensor_copy(out=gg[:], in_=graw[G][:].rearrange("p t n -> p n t"))
-            elif eng == "G":
-                nc.gpsimd.tensor_scalar(out=gg[:], in0=graw[G][:].rearrange("p t n -> p n t"), scalar1=1.0, scalar2=0.0, op0=ALU.mult, op1=ALU.add)
-            else:
-                S.copy(out=gg[:], in_=graw[G][:].rearrange("p t n -> p n t"))
-
-        def gquant(G):
-            V.quantize_mx(out=gq[:, G, :].bitcast(FP8X4), scales=gqs[:, G, :], in_=st["gg", G][:].rearrange("p n t -> p (n t)"))
-
-        def zmul(m, G):
-            z = psum.tile([P, 512], F32, name="z", tag="z", bufs=3)
-            st["z", m, G] = z
-            PE.matmul_mx(out=z[:], lhsT=pw[:, 256 * m:256 * (m + 1)].bitcast(FP4X4), lhsT_scale=psc[:, P * m:P * (m + 1)],
-                         rhs=xq[:, G, :].bitcast(FP8X4), rhs_scale=xqs[:, G, :], start=True, stop=True)
-
-        def tanh(m, G):
-            if ("s", m) not in st:
-                st["s", m] = work.tile([P, 2048], F32, name="s", bufs=6, align_bytes=64)
-            S.activation(out=st["s", m][:, 512 * G:512 * (G + 1)], in_=st["z", m, G][:], func=ACT.Tanh, bias=hb[:, m:m + 1], scale=0.5)
-
-        def sturn(m, G):
-            t_ps = psum.tile([P, 4, P], F32, name="sturn", tag="tr", bufs=3)
-            st["tr", m, G] = t_ps
-            for t in range(4):
-                PE.transpose(t_ps[:, t, :], st["s", m][:, 512 * G + P * t:512 * G + P * (t + 1)], ident_f[:])
-
-        def smul(m, G):
-            if ("sw", m) not in st:
-                st["sw", m] = work.tile([P, 2048], BF16, name="sw", bufs=6, align_bytes=64)
-            o = st["sw", m][:, 512 * G:512 * (G + 1)].rearrange("p (m t) -> p m t", t=4)
-            V.tensor_tensor(out=o, in0=st["tr", m, G][:].rearrange("p t m -> p m t"),
-                            in1=wh[:, G:G + 1, :].to_broadcast([P, P, 4]), op=ALU.mult)
-
-        def hdiff(m, G0=0, G1=NG):
-            o = hds[:, m:m + 1] if G1 - G0 == NG else hdp[:, m, G0 // 2:G0 // 2 + 1]
-            V.scalar_tensor_tensor(out=junk[:, 512 * G0:512 * G1], in0=st["s", m][:, 512 * G0:512 * G1], scalar=1.0, in1=h_all[:, 512 * G0:512 * G1],
-                                   op0=ALU.mult, op1=ALU.mult, accum_out=o)
-
-        def squant(m):
-            V.quantize_mx(out=swq[m][:].bitcast(FP8X4), scales=sws[m][:], in_=st["sw", m][:])
-
-        def hjoin(i):
-            V.tensor_reduce(out=hds[:, 0:4], in_=hdp[:], axis=AX.X, op=ALU.add)
-
-        def alpha_a(m0, m1):
-            V.tensor_scalar(out=al1[:, m0:m1], in0=hds[:, m0:m1], scalar1=sc[:, 3:4], scalar2=2.0, op0=ALU.mult, op1=ALU.add)
-
-        def alpha_b(m0, m1):
-            V.scalar_tensor_tensor(out=al2[:, m0:m1], in0=hds[:, m0:m1], scalar=sc[:, 1:2], in1=al1[:, m0:m1], op0=ALU.add, op1=ALU.mult)
-
-        def aroot(m0, m1):
-            r = roots[m0]
-            nc.gpsimd.tensor_tensor(out=r[:, 0:m1 - m0], in0=al2[:, m0:m1], in1=pows[:, 0:m1 - m0], op=ALU.pow)
-            for m in range(m0, m1):
-                st["root", m] = r[:, m - m0:m - m0 + 1]
-
-        def arecip(m0, m1):
-            V.reciprocal(out=al3[:], in_=al2[:, m0:m1])
-
-        def dmul(m, cols=((0, T),)):
-            d = psum.tile([P, T], F32, name="d", tag="d", bufs=2)
-            st["d", m] = d
-            for c0, c1 in cols:
-                for G in range(NG):
-                    PE.matmul_mx(out=d[:, c0:c1], lhsT=swq[m][:, P * G:P * (G + 1)].bitcast(FP8X4), lhsT_scale=sws[m][:, P * G:P * (G + 1)],
-                                 rhs=gq[:, G, c0:c1].bitcast(FP8X4), rhs_scale=gqs[:, G, c0:c1], start=(G == 0), stop=(G == NG - 1))
-
-        def tile3(kind, m):
-            if (kind, m) not in st:
-                st[kind, m] = work.tile([P, T], F32, name=kind, bufs=3)
-            return st[kind, m]
-
-        def ushift(m, c0=0, c1=T):
-            V.scalar_tensor_tensor(out=tile3("u", m)[:, c0:c1], in0=gtn[:, c0:c1], scalar=hds[:, m:m + 1], in1=st["d", m][:, c0:c1], op0=ALU.mult, op1=ALU.add)
-
-        def usq(m, c0=0, c1=T):
-            S.activation(out=tile3("q", m)[:, c0:c1], in_=st["u", m][:, c0:c1], func=ACT.Square, scale=st["root", m] if m < NM - 1 else 1.0)
-
-        def vfin(m):
-            o = tile3("o", m)
-            V.tensor_tensor(out=o[:], in0=st["q", m][:], in1=erow[:], op=ALU.subtract)
-            nc.sync.dma_start(out=out[P * m:P * (m + 1), :], in_=o[:])
-
-        def gfin(m):
-            o = tile3("o", m)
-            nc.gpsimd.tensor_tensor(out=o[:], in0=st["q", m][:], in1=erow[:], op=ALU.subtract)
-            nc.sync.dma_start(out=out[P * m:P * (m + 1), :], in_=o[:])
-
-        def hcp(m, G):
-            if ("sT", m) not in st:
-                st["sT", m] = work.tile([P, 2048], F32, name="sT", bufs=2, align_bytes=64)
-            for t in range(4):
-                S.activation(out=st["sT", m][:, 512 * G + P * t:512 * G + P * (t + 1)], in_=st["tr", m, G][:, t, :], func=ACT.Copy, scale=h_f[:, 4 * G + t:4 * G + t + 1])
-
-        def hmul(m):
-            ha = psum.tile([P, P], F32, name="ha", tag="d", bufs=2)
-            st["ha", m] = ha
-            for i in range(16):
-                PE.matmul(ha[:], lhsT=st["sT", m][:, P * i:P * (i + 1)], rhs=ident_f[:], start=(i == 0), stop=(i == 15), is_transpose=True)
-
-        def hout(m):
-            ha = st["ha", m]
-            V.tensor_reduce(out=hdp[:, m, 0:1] if m < 4 else hds[:, m:m + 1], in_=ha[:], axis=AX.X, op=ALU.add)
-
-        def fin(m, c0=0, c1=T):
-            o = tile3("o", m)
-            V.scalar_tensor_tensor(out=o[:, c0:c1], in0=st["q", m][:, c0:c1], scalar=al3[:], in1=erow[:, c0:c1], op0=ALU.mult, op1=ALU.subtract)
-            nc.sync.dma_start(out=out[P * m:P * (m + 1), c0:c1], in_=o[:, c0:c1])
-
-        def warm_up():
-            if "wm" not in st:
-                st["wm"] = psum.tile([P, 4, P], F32, name="wm", tag="d", bufs=2)
-            PE.matmul(st["wm"][:], lhsT=ident_b[:], rhs=ident_b[:].unsqueeze(1).to_broadcast([P, 4, P]), start=True, stop=True)
+        GP.memset(hd_part[:], 0.0)
+        GP.memset(exponents[:, 0:BY_GROUP], -0.5)
+        GP.memset(exponents[:, BY_GROUP:], -1.0)
+        nc.scalar.dma_start(out=x_sc[:], in_=x_scale.rearrange("(grp r j) q -> r grp (j q)", r=P, j=TILES))
+        for j in (0, 2):
+            nc.sync.dma_start(out=x_raw[0][:, D * j:D * (j + 2)], in_=x_view[0][:, D * j:D * (j + 2)])
+        nc.scalar.dma_start(out=rows[0:NG, 0:GROUP], in_=w.rearrange("(grp f) -> grp f", grp=NG))
+        nc.scalar.dma_start(out=rows[NG:2 * NG, 0:GROUP], in_=h.rearrange("(grp f) -> grp f", grp=NG))
+        nc.scalar.dma_start(out=rows[0:NM, GROUP:], in_=b.rearrange("(mt c) -> mt c", c=P))
+        S.activation(out=first_tanh[:], in_=first_tanh[:], func=ACT.Tanh)
+        nc.sync.dma_start(out=x_raw[1][:], in_=x_view[1])
+        nc.sync.dma_start(out=p_q[:].bitcast(I32), in_=p_words[0].bitcast(I32))
+        for grp in range(2, NG):
+            nc.sync.dma_start(out=x_raw[grp][:], in_=x_view[grp])
+        nc.sync.dma_start(out=g_raw[0][:], in_=g_view[0])
+        for c in range(4):
+            nc.sync.dma_start(out=p_q_sc[32 * c:32 * c + 4, :].bitcast(I32), in_=p_scales[0, 4 * c:4 * c + 4, :].bitcast(I32))
+        for grp in range(1, NG):
+            nc.sync.dma_start(out=g_raw[grp][:], in_=g_view[grp])
 
         def turn_rows():
-            t_ps = psum.tile([P, 5, P], BF16, name="rt", tag="tr", bufs=3)
-            for t in range(4):
-                PE.transpose(t_ps[:, t, :], rows[:, t:512:4], ident_b[:])
-            PE.transpose(t_ps[:, 4, :], rows[:, 512:640], ident_b[:])
-            st["rt"] = t_ps
+            bank = turn_bank([P, TILES + 1, P], BF16, "rows_turned")
+            live["rows"] = bank
+            for j in range(TILES):
+                PE.transpose(bank[:, j, :], rows[:, j:GROUP:TILES], ident_b[:])
+            PE.transpose(bank[:, TILES, :], rows[:, GROUP:], ident_b[:])
 
-        def rows_out():
-            t_ps = st["rt"]
-            V.tensor_copy(out=wh[:], in_=t_ps[:, 0:4, 0:8].rearrange("p t c -> p c t"))
-            V.tensor_copy(out=h_f[:].rearrange("p (c t) -> p c t", t=4), in_=wh[:, 4:8, :])
-            V.tensor_scalar(out=hb[:], in0=t_ps[:, 4, 0:8], scalar1=0.5, scalar2=None, op0=ALU.mult)
+        def take_rows():
+            bank = live["rows"]
+            V.tensor_copy(out=wh[:], in_=bank[:, 0:TILES, 0:2 * NG].rearrange("r j c -> r c j"))
+            V.tensor_copy(out=h_col[:].rearrange("r (c j) -> r c j", j=TILES), in_=wh[:, NG:, :])
+            V.tensor_scalar(out=b_half[:], in0=bank[:, TILES, 0:NM], scalar1=0.5, scalar2=None, op0=ALU.mult)
 
-        def hspread(G):
-            t_ps = psum.tile([P, 512], F32, name="hs", tag="tr" if G < 2 else "d", bufs=3 if G < 2 else 2)
-            st["hs", G] = t_ps
-            for t in range(4):
-                PE.matmul(t_ps[:, P * t:P * (t + 1)], lhsT=wh[:, 4 + G, t:t + 1].to_broadcast([P, P]), rhs=ident_b[:], start=True, stop=True)
+        def spread_h(grp):
+            bank = turn_bank([P, GROUP], F32, "h_spread") if grp < 2 else other_bank([P, GROUP], "h_spread")
+            live["h", grp] = bank
+            for j in range(TILES):
+                column = wh[:, NG + grp, j:j + 1].to_broadcast([P, P])
+                PE.matmul(bank[:, P * j:P * (j + 1)], lhsT=column, rhs=ident_b[:], start=True, stop=True)
 
-        def hcopy(G):
-            S.activation(out=h_all[:, 512 * G:512 * (G + 1)], in_=st["hs", G][:], func=ACT.Copy, accum_out=ht4[:, G:G + 1])
-
-        def gtotal(G):
-            if G == 0:
-                st["gt"] = psum.tile([P, T], F32, name="gt", tag="d", bufs=2)
-            for t in range(4):
-                PE.matmul(st["gt"][:], lhsT=wh[:, G, t:t + 1].to_broadcast([P, P]), rhs=graw[G][:, t, :], start=(G == 0 and t == 0), stop=(G == NG - 1 and t == 3))
+        def copy_h(grp):
+            S.activation(out=h_row[:, GROUP * grp:GROUP * (grp + 1)], in_=live["h", grp][:], func=ACT.Copy, accum_out=ht_part[:, grp:grp + 1])
 
         def totals():
-            GP = nc.gpsimd
-            V.tensor_reduce(out=sc[:, 0:1], in_=ht4[:], axis=AX.X, op=ALU.add)
-            GP.tensor_scalar(out=sc[:, 1:2], in0=sc[:, 0:1], scalar1=1.0, scalar2=2.0 * LAM, op0=ALU.mult, op1=ALU.add)
-            GP.tensor_tensor(out=sc[:, 2:3], in0=sc[:, 1:2], in1=pows[:, 4:5], op=ALU.pow)
-            GP.tensor_scalar(out=sc[:, 3:4], in0=sc[:, 2:3], scalar1=-2.0, scalar2=0.0, op0=ALU.mult, op1=ALU.add)
-            GP.tensor_scalar(out=sc[:, 4:5], in0=sc[:, 2:3], scalar1=-1.0, scalar2=0.0, op0=ALU.mult, op1=ALU.add)
-            GP.tensor_scalar(out=sc[:, 5:6], in0=sc[:, 0:1], scalar1=LAM, scalar2=sc[:, 1:2], op0=ALU.add, op1=ALU.mult)
-            GP.tensor_tensor(out=sc[:, 6:7], in0=sc[:, 5:6], in1=pows[:, 4:5], op=ALU.pow)
-            GP.tensor_scalar(out=sc[:, 7:8], in0=sc[:, 6:7], scalar1=0.5 * LAM, scalar2=0.0, op0=ALU.mult, op1=ALU.add)
+            V.tensor_reduce(out=ht[:], in_=ht_part[:], axis=AX.X, op=ALU.add)
+            GP.tensor_scalar(out=s_sum[:], in0=ht[:], scalar1=1.0, scalar2=2.0 * LAM, op0=ALU.mult, op1=ALU.add)
+            GP.tensor_tensor(out=s_inv[:], in0=s_sum[:], in1=exponents[:, BY_GROUP:], op=ALU.pow)
+            GP.tensor_scalar(out=s_m2inv[:], in0=s_inv[:], scalar1=-2.0, scalar2=0.0, op0=ALU.mult, op1=ALU.add)
+            GP.tensor_scalar(out=s_m1inv[:], in0=s_inv[:], scalar1=-1.0, scalar2=0.0, op0=ALU.mult, op1=ALU.add)
+            GP.tensor_scalar(out=e_den[:], in0=ht[:], scalar1=LAM, scalar2=s_sum[:], op0=ALU.add, op1=ALU.mult)
+            GP.tensor_tensor(out=e_inv[:], in0=e_den[:], in1=exponents[:, BY_GROUP:], op=ALU.pow)
+            GP.tensor_scalar(out=e_fac[:], in0=e_inv[:], scalar1=0.5 * LAM, scalar2=0.0, op0=ALU.mult, op1=ALU.add)
 
-        def gt_rows_s():
-            S.activation(out=gt2[:], in_=st["gt"][:], func=ACT.Square)
-            S.activation(out=gtn[:], in_=st["gt"][:], func=ACT.Copy, scale=sc[:, 4:5])
+        def total_g(i):
+            if i == 0:
+                live["gt"] = other_bank([P, T], "gt")
+            grp, j = i // TILES, i % TILES
+            PE.matmul(live["gt"][:], lhsT=wh[:, grp, j:j + 1].to_broadcast([P, P]), rhs=g_raw[grp][:, j, :], start=i == 0, stop=i == NG * TILES - 1)
 
-        def gt_rows_v():
-            V.tensor_scalar(out=erow[:], in0=gt2[:], scalar1=sc[:, 7:8], scalar2=None, op0=ALU.mult)
+        def take_gt():
+            S.activation(out=gt_sq[:], in_=live["gt"][:], func=ACT.Square)
+            S.activation(out=gt_shift[:], in_=live["gt"][:], func=ACT.Copy, scale=s_m1inv[:])
 
-        xprod(0, 3, "S")
-        xprod(0, 0, "V")
-        xprod(0, 2, "V")
-        xprod(0, 1, "V")
-        xprod(1, 2, "V")
-        xprod(1, 1, "S")
-        warm_up()
-        warm_up()
-        warm_up()
-        warm_up()
-        warm_up()
+        def make_last_term():
+            V.tensor_scalar(out=last_term[:], in0=gt_sq[:], scalar1=e_fac[:], scalar2=None, op0=ALU.mult)
+
+        def scale_x(grp, j, eng):
+            x_bf = handed(("x_bf", grp), lambda: work.tile([P, TILES, D], BF16, name="x_bf", bufs=4, align_bytes=64))
+            for q in range(SCALES):
+                at = slice(P * q, P * (q + 1))
+                values = x_raw[grp][:, D * j + P * q:D * j + P * (q + 1)].bitcast(FP8)
+                scale = x_sc[:, grp, SCALES * j + q:SCALES * j + q + 1]
+                if eng is V:
+                    V.tensor_scalar(out=x_bf[:, j, at], in0=values, scalar1=scale, scalar2=None, op0=ALU.mult)
+                else:
+                    S.activation(out=x_bf[:, j, at], in_=values, func=ACT.Copy, scale=scale)
+
+        def turn_x(grp, half):
+            bank = other_bank([P, 2, 2, P], "x_turned")
+            live["x_turned", grp, half] = bank
+            for i in range(2):
+                words = live["x_bf", grp][:, 2 * half + i, :].bitcast(F32)
+                for u in range(2):
+                    PE.transpose(bank[:, i, u, :], words[:, u:D // 2:2], ident_f[:])
+
+        def copy_x(grp, half, eng):
+            mixed = handed(("x_mixed", grp), lambda: work.tile([P, GROUP * TILES], BF16, name="x_mixed", bufs=3, align_bytes=64))
+            words = mixed[:, HALF_GROUP * TILES * half:HALF_GROUP * TILES * (half + 1)].bitcast(F32)
+            target = words.rearrange("p (i r u) -> p i r u", i=2, u=2)
+            source = live["x_turned", grp, half][:].rearrange("p i u r -> p i r u")
+            if eng is V:
+                V.tensor_copy(out=target, in_=source)
+            else:
+                S.copy(out=target, in_=source)
+
+        def quantise_x(grp, c0=0, c1=GROUP):
+            V.quantize_mx(out=x_q[:, grp, c0:c1].bitcast(FP8X4), scales=x_q_sc[:, grp, c0:c1], in_=live["x_mixed", grp][:, TILES * c0:TILES * c1])
+
+        def mix_g(grp, eng):
+            mixed = work.tile([P, T, TILES], BF16, name="g_mixed", bufs=3, align_bytes=64)
+            live["g_mixed", grp] = mixed
+            source = g_raw[grp][:].rearrange("r j t -> r t j")
+            if eng is V:
+                V.tensor_copy(out=mixed[:], in_=source)
+            elif eng is GP:
+                GP.tensor_scalar(out=mixed[:], in0=source, scalar1=1.0, scalar2=0.0, op0=ALU.mult, op1=ALU.add)
+            else:
+                S.copy(out=mixed[:], in_=source)
+
+        def quantise_g(grp):
+            V.quantize_mx(out=g_q[:, grp, :].bitcast(FP8X4), scales=g_q_sc[:, grp, :], in_=live["g_mixed", grp][:].rearrange("r t j -> r (t j)"))
+
+        def make_z(mt, grp):
+            z = z_bank()
+            live["z", mt, grp] = z
+            PE.matmul_mx(
+                out=z[:],
+                lhsT=p_q[:, 2 * P * mt:2 * P * (mt + 1)].bitcast(FP4X4),
+                lhsT_scale=p_q_sc[:, P * mt:P * (mt + 1)],
+                rhs=x_q[:, grp, :].bitcast(FP8X4),
+                rhs_scale=x_q_sc[:, grp, :],
+                start=True,
+                stop=True,
+            )
+
+        def make_s(mt, grp):
+            s = handed(("s", mt), lambda: work.tile([P, N], F32, name="s", bufs=6, align_bytes=64))
+            S.activation(out=s[:, GROUP * grp:GROUP * (grp + 1)], in_=live["z", mt, grp][:], func=ACT.Tanh, bias=b_half[:, mt:mt + 1], scale=0.5)
+
+        def turn_s(mt, grp):
+            bank = turn_bank([P, TILES, P], F32, "s_turned")
+            live["s_turned", mt, grp] = bank
+            for j in range(TILES):
+                PE.transpose(bank[:, j, :], live["s", mt][:, GROUP * grp + P * j:GROUP * grp + P * (j + 1)], ident_f[:])
+
+        def weigh_s(mt, grp):
+            sw = handed(("sw", mt), lambda: work.tile([P, NG * P * TILES], BF16, name="sw", bufs=6, align_bytes=64))
+            V.tensor_tensor(
+                out=sw[:, GROUP * grp:GROUP * (grp + 1)].rearrange("r (m j) -> r m j", j=TILES),
+                in0=live["s_turned", mt, grp][:].rearrange("r j m -> r m j"),
+                in1=wh[:, grp:grp + 1, :].to_broadcast([P, P, TILES]),
+                op=ALU.mult,
+            )
+
+        def copy_sh(mt, grp):
+            sh = handed(("sh", mt), lambda: work.tile([P, N], F32, name="sh", bufs=2, align_bytes=64))
+            for j in range(TILES):
+                i = TILES * grp + j
+                S.activation(out=sh[:, P * i:P * (i + 1)], in_=live["s_turned", mt, grp][:, j, :], func=ACT.Copy, scale=h_col[:, i:i + 1])
+
+        def hd_by_vector(mt, grp0=0, grp1=NG):
+            total = hd[:, mt:mt + 1] if grp1 - grp0 == NG else hd_part[:, mt, grp0 // 2:grp0 // 2 + 1]
+            at = slice(GROUP * grp0, GROUP * grp1)
+            V.scalar_tensor_tensor(out=product[:, at], in0=live["s", mt][:, at], scalar=1.0, in1=h_row[:, at], op0=ALU.mult, op1=ALU.mult, accum_out=total)
+
+        def hd_by_turns(mt):
+            bank = other_bank([P, P], "hd_turned")
+            live["hd_turned", mt] = bank
+            for i in range(NG * TILES):
+                PE.matmul(bank[:], lhsT=live["sh", mt][:, P * i:P * (i + 1)], rhs=ident_f[:], start=i == 0, stop=i == NG * TILES - 1, is_transpose=True)
+
+        def hd_from_turns(mt):
+            total = hd_part[:, mt, 0:1] if mt < BY_GROUP else hd[:, mt:mt + 1]
+            V.tensor_reduce(out=total, in_=live["hd_turned", mt][:], axis=AX.X, op=ALU.add)
+
+        def join_hd():
+            V.tensor_reduce(out=hd[:, 0:BY_GROUP], in_=hd_part[:], axis=AX.X, op=ALU.add)
+
+        def start_den(mt0, mt1):
+            V.tensor_scalar(out=den_a[:, mt0:mt1], in0=hd[:, mt0:mt1], scalar1=s_m2inv[:], scalar2=2.0, op0=ALU.mult, op1=ALU.add)
+
+        def make_den(mt0, mt1):
+            V.scalar_tensor_tensor(out=den[:, mt0:mt1], in0=hd[:, mt0:mt1], scalar=s_sum[:], in1=den_a[:, mt0:mt1], op0=ALU.add, op1=ALU.mult)
+
+        def root_den(mt0, mt1):
+            root = den_root[mt0]
+            GP.tensor_tensor(out=root[:, 0:mt1 - mt0], in0=den[:, mt0:mt1], in1=exponents[:, 0:mt1 - mt0], op=ALU.pow)
+            for mt in range(mt0, mt1):
+                live["root", mt] = root[:, mt - mt0:mt - mt0 + 1]
+
+        def invert_den(mt):
+            V.reciprocal(out=den_inv[:], in_=den[:, mt:mt + 1])
+
+        def quantise_sw(mt):
+            V.quantize_mx(out=sw_q[mt][:].bitcast(FP8X4), scales=sw_q_sc[mt][:], in_=live["sw", mt][:])
+
+        def make_d(mt, width=T):
+            d = other_bank([P, T], "d")
+            live["d", mt] = d
+            for c0 in range(0, T, width):
+                for grp in range(NG):
+                    PE.matmul_mx(
+                        out=d[:, c0:c0 + width],
+                        lhsT=sw_q[mt][:, P * grp:P * (grp + 1)].bitcast(FP8X4),
+                        lhsT_scale=sw_q_sc[mt][:, P * grp:P * (grp + 1)],
+                        rhs=g_q[:, grp, c0:c0 + width].bitcast(FP8X4),
+                        rhs_scale=g_q_sc[:, grp, c0:c0 + width],
+                        start=grp == 0,
+                        stop=grp == NG - 1,
+                    )
+
+        def row_tile(kind, mt):
+            return handed((kind, mt), lambda: work.tile([P, T], F32, name=kind, bufs=3))
+
+        def shift_d(mt, c0=0, c1=T):
+            V.scalar_tensor_tensor(out=row_tile("shifted", mt)[:, c0:c1], in0=gt_shift[:, c0:c1], scalar=hd[:, mt:mt + 1], in1=live["d", mt][:, c0:c1], op0=ALU.mult, op1=ALU.add)
+
+        def square(mt, c0=0, c1=T):
+            scale = 1.0 if mt == LAST else live["root", mt]
+            S.activation(out=row_tile("squared", mt)[:, c0:c1], in_=live["shifted", mt][:, c0:c1], func=ACT.Square, scale=scale)
+
+        def store(mt, c0, c1):
+            nc.sync.dma_start(out=out[P * mt:P * (mt + 1), c0:c1], in_=live["gain", mt][:, c0:c1])
+
+        def finish(mt, eng):
+            eng.tensor_tensor(out=row_tile("gain", mt)[:], in0=live["squared", mt][:], in1=last_term[:], op=ALU.subtract)
+            store(mt, 0, T)
+
+        def finish_last(c0, c1):
+            gain = row_tile("gain", LAST)
+            V.scalar_tensor_tensor(out=gain[:, c0:c1], in0=live["squared", LAST][:, c0:c1], scalar=den_inv[:], in1=last_term[:, c0:c1], op0=ALU.mult, op1=ALU.subtract)
+            store(LAST, c0, c1)
+
+        units = [(mt, grp) for grp in range(NG) for mt in range(BY_GROUP)] + [(mt, grp) for mt in range(BY_GROUP, NM) for grp in range(NG)]
+
+        scale_x(0, 0, V)
+        scale_x(0, 3, V)
+        scale_x(0, 1, S)
+        scale_x(1, 0, S)
         turn_rows()
-        xturn(0, 1)
-        xturn(0, 0)
-        xcopy(0, 1, "S")
-        rows_out()
-        hspread(1)
-        xprod(2, 3, "V")
-        xprod(1, 0, "V")
-        xquant(0, 256, 512)
-        xprod(3, 0, "V")
-        xcopy(0, 0, "S")
-        xprod(1, 3, "V")
-        xquant(0, 0, 256)
-        xprod(2, 1, "V")
-        xprod(3, 2, "S")
-        hspread(0)
-        xprod(2, 2, "S")
-        xturn(1, 0)
-        xturn(1, 1)
-        xcopy(1, 0, "S")
-        gmix(0, "V")
-        xcopy(1, 1, "S")
-        zmul(0, 0)
-        zmul(1, 0)
-        xquant(1)
-        tanh(0, 0)
-        xprod(2, 0, "V")
-        xturn(2, 1)
-        xprod(3, 1, "V")
-        zmul(2, 0)
-        zmul(3, 0)
-        tanh(1, 0)
-        sturn(0, 0)
-        xcopy(2, 1, "V")
-        tanh(2, 0)
-        hcopy(0)
-        xturn(2, 0)
-        xcopy(2, 0, "V")
-        hcopy(1)
-        zmul(0, 1)
-        zmul(1, 1)
-        tanh(3, 0)
-        sturn(1, 0)
-        sturn(2, 0)
-        smul(0, 0)
-        tanh(0, 1)
-        smul(1, 0)
-        xprod(3, 3, "S")
-        xturn(3, 0)
-        zmul(2, 1)
-        zmul(3, 1)
-        tanh(1, 1)
-        sturn(3, 0)
-        sturn(0, 1)
-        smul(2, 0)
-        hcp(2, 0)
-        xquant(2)
-        gquant(0)
-        tanh(2, 1)
-        smul(3, 0)
-        xturn(3, 1)
-        gmix(1, "G")
-        zmul(0, 2)
-        zmul(1, 2)
-        tanh(3, 1)
-        sturn(1, 1)
-        sturn(2, 1)
-        smul(0, 1)
-        xcopy(3, 0, "S")
-        hdiff(0, 0, 2)
-        xcopy(3, 1, "S")
-        tanh(0, 2)
-        smul(1, 1)
-        xquant(3)
-        hspread(2)
-        hcopy(2)
-        zmul(2, 2)
-        zmul(3, 2)
-        tanh(1, 2)
-        sturn(3, 1)
-        sturn(0, 2)
-        smul(2, 1)
-        hcp(2, 1)
-        hspread(3)
-        gquant(1)
-        tanh(2, 2)
-        smul(3, 1)
-        hdiff(1, 0, 2)
-        zmul(0, 3)
-        zmul(1, 3)
-        tanh(3, 2)
-        sturn(1, 2)
-        sturn(2, 2)
-        smul(0, 2)
-        tanh(0, 3)
-        smul(1, 2)
-        hcopy(3)
-        zmul(2, 3)
-        zmul(3, 3)
-        tanh(1, 3)
-        sturn(3, 2)
-        sturn(0, 3)
-        smul(2, 2)
-        hcp(2, 2)
-        gtotal(0)
-        tanh(2, 3)
-        smul(3, 2)
-        gtotal(1)
-        gmix(3, "S")
-        zmul(4, 0)
-        zmul(4, 1)
-        tanh(3, 3)
-        sturn(1, 3)
-        sturn(2, 3)
-        smul(0, 3)
-        gtotal(2)
-        hdiff(0, 2, 4)
-        squant(0)
-        hdiff(1, 2, 4)
-        tanh(4, 0)
-        smul(1, 3)
-        gquant(3)
-        gmix(2, "G")
-        zmul(4, 2)
-        zmul(4, 3)
-        tanh(4, 1)
-        sturn(3, 3)
-        sturn(4, 0)
-        smul(2, 3)
-        hcp(2, 3)
-        hdiff(3, 2, 4)
-        totals()
-        gtotal(3)
-        hdiff(3, 0, 2)
-        tanh(4, 2)
-        smul(3, 3)
-        gt_rows_s()
-        hmul(2)
-        zmul(5, 0)
-        zmul(5, 1)
-        tanh(4, 3)
-        sturn(4, 1)
-        sturn(4, 2)
-        smul(4, 0)
-        hcp(4, 0)
-        squant(1)
-        gquant(2)
-        tanh(5, 0)
-        smul(4, 1)
-        hcp(4, 1)
-        hout(2)
-        dmul(0)
-        squant(3)
-        hjoin(0)
-        gt_rows_v()
-        zmul(5, 2)
-        zmul(5, 3)
-        tanh(5, 1)
-        sturn(4, 3)
-        sturn(5, 0)
-        smul(4, 2)
-        hcp(4, 2)
-        ushift(0)
-        dmul(1)
-        alpha_a(0, 4)
-        tanh(5, 2)
-        smul(4, 3)
-        hcp(4, 3)
-        alpha_b(0, 4)
-        squant(2)
-        zmul(6, 0)
-        zmul(6, 1)
-        tanh(5, 3)
-        sturn(5, 1)
-        sturn(5, 2)
-        smul(5, 0)
-        hmul(4)
-        aroot(0, 4)
-        ushift(1)
-        usq(0)
-        tanh(6, 0)
-        smul(5, 1)
-        squant(4)
-        zmul(6, 2)
-        zmul(6, 3)
-        tanh(6, 1)
-        sturn(5, 3)
-        sturn(6, 0)
-        smul(5, 2)
-        hout(4)
-        hdiff(5)
-        gfin(0)
-        dmul(2)
-        tanh(6, 2)
-        smul(5, 3)
-        dmul(3)
-        usq(1)
-        gfin(1)
-        zmul(7, 0)
-        zmul(7, 1)
-        tanh(6, 3)
-        sturn(6, 1)
-        sturn(6, 2)
-        smul(6, 0)
-        hcp(6, 0)
-        ushift(2)
-        ushift(3)
-        dmul(4)
-        usq(2)
-        usq(3)
-        tanh(7, 0)
-        smul(6, 1)
-        hcp(6, 1)
-        alpha_a(4, 6)
-        squant(5)
-        vfin(2)
-        gfin(3)
-        zmul(7, 2)
-        zmul(7, 3)
-        tanh(7, 1)
-        sturn(6, 3)
-        sturn(7, 0)
-        smul(6, 2)
-        hcp(6, 2)
-        alpha_b(4, 6)
-        dmul(5)
-        aroot(4, 6)
-        ushift(4)
-        tanh(7, 2)
-        smul(6, 3)
-        hcp(6, 3)
-        squant(6)
-        ushift(5)
-        hmul(6)
-        usq(4)
-        tanh(7, 3)
-        sturn(7, 1)
-        sturn(7, 2)
-        smul(7, 0)
-        hout(6)
-        smul(7, 1)
-        sturn(7, 3)
-        smul(7, 2)
-        smul(7, 3)
-        alpha_a(6, 7)
-        squant(7)
-        hdiff(7)
-        dmul(6)
-        dmul(7, ((0, 256), (256, 512)))
-        alpha_b(6, 7)
-        usq(5)
-        alpha_a(7, 8)
-        ushift(7, 0, 256)
-        gfin(4)
-        usq(7, 0, 256)
-        ushift(6)
-        alpha_b(7, 8)
-        ushift(7, 256, 512)
-        arecip(7, 8)
-        gfin(5)
-        aroot(6, 7)
-        usq(6)
-        fin(7, 0, 256)
-        vfin(6)
-        usq(7, 256, 512)
-        fin(7, 256, 512)
+        scale_x(1, 2, S)
+        turn_x(0, 0)
+        scale_x(0, 2, V)
+        take_rows()
+        scale_x(1, 3, V)
+        scale_x(2, 2, V)
+        copy_x(0, 0, S)
+        turn_x(0, 1)
+        spread_h(0)
+        scale_x(2, 1, V)
+        spread_h(1)
+        scale_x(2, 3, V)
+        scale_x(2, 0, S)
+        scale_x(3, 2, V)
+        quantise_x(0, 0, HALF_GROUP)
+        copy_x(0, 1, S)
+        scale_x(1, 1, S)
+        turn_x(1, 1)
+        turn_x(1, 0)
+        quantise_x(0, HALF_GROUP, GROUP)
+        scale_x(3, 1, V)
+        mix_g(0, V)
+
+        between = {
+            -4: [(copy_h, 0), (scale_x, 3, 0, V), (copy_x, 1, 1, S)],
+            -3: [(quantise_g, 0), (copy_x, 1, 0, S)],
+            -2: [(turn_x, 2, 0), (copy_h, 1)],
+            -1: [(quantise_x, 1), (copy_x, 2, 0, V), (scale_x, 3, 3, S), (turn_x, 2, 1)],
+            0: [(copy_x, 2, 1, V), (mix_g, 1, GP)],
+            2: [(turn_x, 3, 0), (turn_x, 3, 1), (quantise_x, 2)],
+            3: [(copy_x, 3, 0, S)],
+            4: [(quantise_g, 1), (spread_h, 2), (hd_by_vector, 0, 0, 2)],
+            5: [(copy_x, 3, 1, S), (copy_h, 2)],
+            6: [(quantise_x, 3), (hd_by_vector, 1, 0, 2)],
+            7: [(spread_h, 3), (total_g, 0), (total_g, 1)],
+            8: [(mix_g, 2, GP)],
+            9: [(copy_h, 3)],
+            10: [(total_g, 2), (total_g, 3), (totals,)],
+            11: [(total_g, 4), (total_g, 5), (hd_by_vector, 1, 2, 4), (total_g, 6)],
+            12: [(total_g, 7), (total_g, 8), (hd_by_vector, 3, 2, 4), (total_g, 9), (total_g, 10)],
+            13: [(total_g, 11), (total_g, 12), (mix_g, 3, S)],
+            14: [(quantise_sw, 0), (hd_by_turns, 2), (total_g, 13), (quantise_g, 2)],
+            15: [(quantise_g, 3), (total_g, 14), (hd_by_vector, 0, 2, 4), (total_g, 15), (take_gt,)],
+            16: [(make_d, 0), (quantise_sw, 1)],
+            17: [(hd_by_vector, 3, 0, 2), (hd_from_turns, 2)],
+            18: [(join_hd,), (quantise_sw, 2), (start_den, 0, 4), (make_d, 1)],
+            19: [(make_last_term,), (shift_d, 0)],
+            20: [(make_den, 0, 4), (hd_by_turns, 4), (shift_d, 1)],
+            21: [(quantise_sw, 3), (make_d, 2), (root_den, 0, 4), (square, 1), (hd_by_vector, 5)],
+            22: [(hd_from_turns, 4), (quantise_sw, 4)],
+            23: [(make_d, 3), (square, 0)],
+            24: [(finish, 1, GP), (shift_d, 2), (square, 2), (shift_d, 3)],
+            25: [(make_d, 4), (start_den, 4, 6), (finish, 0, GP), (quantise_sw, 5)],
+            26: [(finish, 2, GP), (square, 3), (make_den, 4, 6), (shift_d, 4)],
+            27: [(root_den, 4, 6), (square, 4), (make_d, 5), (finish, 3, V), (quantise_sw, 6), (hd_by_turns, 6), (shift_d, 5)],
+            30: [(square, 5), (hd_from_turns, 6)],
+            31: [(start_den, 6, 7)],
+        }
+
+        for i in range(-4, len(units)):
+            pair = (i, i + 1) if i % 2 == 0 else ()
+            for k in pair:
+                if k + 4 < len(units):
+                    make_z(*units[k + 4])
+            if 0 <= i + 3 < len(units):
+                make_s(*units[i + 3])
+            for k in pair:
+                if 0 <= k + 1 < len(units):
+                    turn_s(*units[k + 1])
+            if i >= 0:
+                mt, grp = units[i]
+                weigh_s(mt, grp)
+                if mt in TURNED:
+                    copy_sh(mt, grp)
+            for piece in between.get(i, ()):
+                piece[0](*piece[1:])
+
+        quantise_sw(7)
+        hd_by_vector(7)
+        make_den(6, 7)
+        finish(4, GP)
+        start_den(7, 8)
+        make_d(6)
+        make_d(LAST, T // 2)
+        finish(5, GP)
+        root_den(6, 7)
+        shift_d(LAST, 0, T // 2)
+        make_den(7, 8)
+        square(LAST, 0, T // 2)
+        shift_d(6)
+        square(6)
+        invert_den(LAST)
+        shift_d(LAST, T // 2, T)
+        finish_last(0, T // 2)
+        finish(6, V)
+        square(LAST, T // 2, T)
+        finish_last(T // 2, T)

@@ -248,7 +248,7 @@ def tile_obliquesoftsplitgaintable_d1p_kernel(tc, x_bytes, x_scale, p_words, p_s
                 S.activation(out=sh[:, P * i:P * (i + 1)], in_=live["s_turned", mt, grp][:, j, :], func=ACT.Copy, scale=h_col[:, i:i + 1])
 
         def hd_by_vector(mt, grp0=0, grp1=NG):
-            total = hd[:, mt:mt + 1] if grp1 - grp0 == NG else hd_part[:, mt, grp0 // 2:grp0 // 2 + 1]
+            total = hd_part[:, mt, grp0 // 2:grp0 // 2 + 1] if mt < BY_GROUP else hd[:, mt:mt + 1]
             at = slice(GROUP * grp0, GROUP * grp1)
             V.scalar_tensor_tensor(out=product[:, at], in0=live["s", mt][:, at], scalar=1.0, in1=h_row[:, at], op0=ALU.mult, op1=ALU.mult, accum_out=total)
 
@@ -322,68 +322,70 @@ def tile_obliquesoftsplitgaintable_d1p_kernel(tc, x_bytes, x_scale, p_words, p_s
 
         units = [(mt, grp) for grp in range(NG) for mt in range(BY_GROUP)] + [(mt, grp) for mt in range(BY_GROUP, NM) for grp in range(NG)]
 
-        scale_x(0, 0, V)
-        scale_x(0, 3, V)
-        scale_x(0, 1, S)
-        scale_x(1, 0, S)
-        turn_rows()
-        scale_x(1, 2, S)
-        turn_x(0, 0)
+        scale_x(0, 0, S)
+        scale_x(0, 1, V)
         scale_x(0, 2, V)
-        take_rows()
-        scale_x(1, 3, V)
-        scale_x(2, 2, V)
-        copy_x(0, 0, S)
+        turn_rows()
+        scale_x(0, 3, S)
+        scale_x(1, 0, S)
         turn_x(0, 1)
-        spread_h(0)
-        scale_x(2, 1, V)
+        turn_x(0, 0)
+        scale_x(1, 2, V)
+        scale_x(1, 3, V)
+        take_rows()
         spread_h(1)
-        scale_x(2, 3, V)
-        scale_x(2, 0, S)
-        scale_x(3, 2, V)
-        quantise_x(0, 0, HALF_GROUP)
         copy_x(0, 1, S)
+        spread_h(0)
+        copy_x(0, 0, S)
+        scale_x(2, 3, V)
+        scale_x(3, 2, V)
+        scale_x(2, 2, V)
+        scale_x(2, 0, S)
+        scale_x(2, 1, V)
+        quantise_x(0)
         scale_x(1, 1, S)
+        copy_h(0)
         turn_x(1, 1)
-        turn_x(1, 0)
-        quantise_x(0, HALF_GROUP, GROUP)
-        scale_x(3, 1, V)
         mix_g(0, V)
+        scale_x(3, 1, V)
+        scale_x(3, 0, S)
+        copy_x(1, 1, S)
+        turn_x(1, 0)
 
         between = {
-            -4: [(copy_h, 0), (scale_x, 3, 0, V), (copy_x, 1, 1, S)],
-            -3: [(quantise_g, 0), (copy_x, 1, 0, S)],
-            -2: [(turn_x, 2, 0), (copy_h, 1)],
-            -1: [(quantise_x, 1), (copy_x, 2, 0, V), (scale_x, 3, 3, S), (turn_x, 2, 1)],
-            0: [(copy_x, 2, 1, V), (mix_g, 1, GP)],
-            2: [(turn_x, 3, 0), (turn_x, 3, 1), (quantise_x, 2)],
-            3: [(copy_x, 3, 0, S)],
-            4: [(quantise_g, 1), (spread_h, 2), (hd_by_vector, 0, 0, 2)],
-            5: [(copy_x, 3, 1, S), (copy_h, 2)],
-            6: [(quantise_x, 3), (hd_by_vector, 1, 0, 2)],
-            7: [(spread_h, 3), (total_g, 0), (total_g, 1)],
+            -4: [(quantise_g, 0), (turn_x, 2, 1)],
+            -3: [(scale_x, 3, 3, S)],
+            -2: [(copy_x, 1, 0, V), (turn_x, 2, 0)],
+            -1: [(copy_h, 1), (quantise_x, 1)],
+            0: [(copy_x, 2, 1, S), (copy_x, 2, 0, V), (turn_x, 3, 0), (mix_g, 1, GP)],
+            2: [(quantise_x, 2), (turn_x, 3, 1), (hd_by_vector, 0, 0, 2)],
+            3: [(quantise_g, 1)],
+            4: [(copy_x, 3, 0, S), (spread_h, 2), (copy_x, 3, 1, S)],
+            5: [(total_g, 0), (copy_h, 2)],
+            6: [(quantise_x, 3), (total_g, 1), (total_g, 2)],
+            7: [(total_g, 3), (spread_h, 3), (hd_by_vector, 1, 0, 2)],
             8: [(mix_g, 2, GP)],
             9: [(copy_h, 3)],
-            10: [(total_g, 2), (total_g, 3), (totals,)],
-            11: [(total_g, 4), (total_g, 5), (hd_by_vector, 1, 2, 4), (total_g, 6)],
-            12: [(total_g, 7), (total_g, 8), (hd_by_vector, 3, 2, 4), (total_g, 9), (total_g, 10)],
-            13: [(total_g, 11), (total_g, 12), (mix_g, 3, S)],
-            14: [(quantise_sw, 0), (hd_by_turns, 2), (total_g, 13), (quantise_g, 2)],
-            15: [(quantise_g, 3), (total_g, 14), (hd_by_vector, 0, 2, 4), (total_g, 15), (take_gt,)],
-            16: [(make_d, 0), (quantise_sw, 1)],
-            17: [(hd_by_vector, 3, 0, 2), (hd_from_turns, 2)],
-            18: [(join_hd,), (quantise_sw, 2), (start_den, 0, 4), (make_d, 1)],
-            19: [(make_last_term,), (shift_d, 0)],
-            20: [(make_den, 0, 4), (hd_by_turns, 4), (shift_d, 1)],
-            21: [(quantise_sw, 3), (make_d, 2), (root_den, 0, 4), (square, 1), (hd_by_vector, 5)],
-            22: [(hd_from_turns, 4), (quantise_sw, 4)],
-            23: [(make_d, 3), (square, 0)],
-            24: [(finish, 1, GP), (shift_d, 2), (square, 2), (shift_d, 3)],
-            25: [(make_d, 4), (start_den, 4, 6), (finish, 0, GP), (quantise_sw, 5)],
-            26: [(finish, 2, GP), (square, 3), (make_den, 4, 6), (shift_d, 4)],
-            27: [(root_den, 4, 6), (square, 4), (make_d, 5), (finish, 3, V), (quantise_sw, 6), (hd_by_turns, 6), (shift_d, 5)],
-            30: [(square, 5), (hd_from_turns, 6)],
-            31: [(start_den, 6, 7)],
+            10: [(totals,), (total_g, 4)],
+            11: [(total_g, 5), (total_g, 6)],
+            12: [(total_g, 7), (hd_by_vector, 1, 2, 4), (total_g, 8), (total_g, 9), (quantise_sw, 0)],
+            13: [(mix_g, 3, S)],
+            14: [(total_g, 10), (quantise_sw, 1), (total_g, 11), (hd_by_vector, 3), (total_g, 12), (total_g, 13), (total_g, 14)],
+            15: [(total_g, 15), (hd_by_vector, 0, 2, 4), (quantise_g, 3), (take_gt,)],
+            16: [(hd_by_turns, 2), (quantise_g, 2)],
+            17: [(hd_from_turns, 2), (make_d, 0), (make_last_term,), (join_hd,)],
+            18: [(start_den, 0, 4), (quantise_sw, 3)],
+            19: [(make_d, 1)],
+            20: [(quantise_sw, 2), (quantise_sw, 4)],
+            21: [(make_den, 0, 4), (shift_d, 1), (root_den, 0, 4), (shift_d, 0)],
+            22: [(square, 0), (make_d, 2)],
+            23: [(hd_by_vector, 5), (square, 1), (hd_by_turns, 4)],
+            24: [(hd_from_turns, 4), (make_d, 3), (shift_d, 2), (square, 2), (make_d, 4), (quantise_sw, 5)],
+            25: [(finish, 0, GP), (finish, 2, GP), (start_den, 4, 6), (make_den, 4, 6)],
+            26: [(root_den, 4, 6), (shift_d, 3), (make_d, 5), (finish, 1, GP), (shift_d, 4), (square, 3)],
+            27: [(square, 4), (hd_by_turns, 6)],
+            28: [(finish, 3, V), (quantise_sw, 6), (shift_d, 5)],
+            30: [(hd_from_turns, 6)],
         }
 
         for i in range(-4, len(units)):
@@ -404,22 +406,24 @@ def tile_obliquesoftsplitgaintable_d1p_kernel(tc, x_bytes, x_scale, p_words, p_s
             for piece in between.get(i, ()):
                 piece[0](*piece[1:])
 
+        start_den(6, 7)
         quantise_sw(7)
         hd_by_vector(7)
         make_den(6, 7)
-        finish(4, GP)
         start_den(7, 8)
         make_d(6)
-        make_d(LAST, T // 2)
+        square(5)
+        finish(4, GP)
         finish(5, GP)
-        root_den(6, 7)
+        make_d(LAST, T // 2)
         shift_d(LAST, 0, T // 2)
         make_den(7, 8)
         square(LAST, 0, T // 2)
         shift_d(6)
-        square(6)
         invert_den(LAST)
         shift_d(LAST, T // 2, T)
+        root_den(6, 7)
+        square(6)
         finish_last(0, T // 2)
         finish(6, V)
         square(LAST, T // 2, T)

from contextlib import ExitStack

import concourse.mybir as mybir
from concourse.masks import make_identity

N, D, M, T = 2048, 512, 1024, 512
P = 128
GROUP = 512
NG = N // GROUP
NM = M // P
TILES = GROUP // P
SCALES = D // P
HALF_GROUP = GROUP // 2
LAST = NM - 1
LAM = 64.0
BY_GROUP = 4
TURNED = (2, 4, 6)
FLOPS = 2 * N * D * M + 2 * N * M * T + 2 * N * T + 2 * N * M

F32 = mybir.dt.float32
BF16 = mybir.dt.bfloat16
U32 = mybir.dt.uint32
I32 = mybir.dt.int32
U8 = mybir.dt.uint8
FP8 = mybir.dt.float8_e4m3fn
FP8X4 = mybir.dt.float8_e4m3fn_x4
FP4X4 = mybir.dt.float4_e2m1fn_x4
ALU = mybir.AluOpType
ACT = mybir.ActivationFunctionType
AX = mybir.AxisListType


def tile_obliquesoftsplitgaintable_d1p_kernel(tc, x_bytes, x_scale, p_words, p_scales, b, w, g, h, out):
    nc = tc.nc
    V, S, PE, GP = nc.vector, nc.scalar, nc.tensor, nc.gpsimd
    with ExitStack() as ctx:
        keep_pool = ctx.enter_context(tc.tile_pool(name="keep", bufs=1))
        work = ctx.enter_context(tc.tile_pool(name="work", bufs=2))
        psum = ctx.enter_context(tc.psum_pool(name="psum", bufs=2))
        ctx.enter_context(tc.manual_schedule())

        def keep(shape, dtype, name):
            return keep_pool.tile(shape, dtype, name=name, align_bytes=64)

        def z_bank():
            return psum.tile([P, GROUP], F32, name="z", tag="z", bufs=3)

        def turn_bank(shape, dtype, name):
            return psum.tile(shape, dtype, name=name, tag="turn", bufs=3)

        def other_bank(shape, name):
            return psum.tile(shape, F32, name=name, tag="other", bufs=2)

        ident_f = keep([P, P], F32, "ident_f")
        ident_b = keep([P, P], BF16, "ident_b")
        x_raw = [keep([P, TILES * D], U8, "x_raw%d" % grp) for grp in range(NG)]
        x_sc = keep([P, NG, TILES * SCALES], F32, "x_sc")
        x_q = keep([P, NG, GROUP], U32, "x_q")
        x_q_sc = keep([P, NG, GROUP], U8, "x_q_sc")
        p_q = keep([P, 2 * M], U8, "p_q")
        p_q_sc = keep([P, M], U8, "p_q_sc")
        rows = keep([P, GROUP + P], BF16, "rows")
        wh = keep([P, 2 * NG, TILES], BF16, "wh")
        h_col = keep([P, NG * TILES], F32, "h_col")
        b_half = keep([P, NM], F32, "b_half")
        h_row = keep([P, N], BF16, "h_row")
        ht_part = keep([P, NG], F32, "ht_part")
        ht, s_sum, s_inv, s_m2inv, s_m1inv, e_den, e_inv, e_fac = [keep([P, 1], F32, "total%d" % i) for i in range(8)]
        g_raw = [keep([P, TILES, T], BF16, "g_raw%d" % grp) for grp in range(NG)]
        g_q = keep([P, NG, T], U32, "g_q")
        g_q_sc = keep([P, NG, T], U8, "g_q_sc")
        gt_shift = keep([P, T], F32, "gt_shift")
        gt_sq = keep([P, T], F32, "gt_sq")
        last_term = keep([P, T], F32, "last_term")
        hd_part = keep([P, BY_GROUP, 2], F32, "hd_part")
        hd = keep([P, NM], F32, "hd")
        den_a = keep([P, NM], F32, "den_a")
        den = keep([P, NM], F32, "den")
        den_root = {mt: keep([P, BY_GROUP], F32, "den_root%d" % mt) for mt in (0, 4, 6)}
        den_inv = keep([P, 1], F32, "den_inv")
        exponents = keep([P, BY_GROUP + 1], F32, "exponents")
        first_tanh = keep([P, 1], F32, "first_tanh")
        product = keep([P, N], BF16, "product")
        sw_q = [keep([P, NG * P], U32, "sw_q%d" % mt) for mt in range(NM)]
        sw_q_sc = [keep([P, NG * P], U8, "sw_q_sc%d" % mt) for mt in range(NM)]
        live = {}

        def handed(key, make):
            if key not in live:
                live[key] = make()
            return live[key]

        x_view = x_bytes.rearrange("(grp r j) k -> grp r (j k)", r=P, j=TILES)
        g_view = g.rearrange("(grp r j) t -> grp r j t", r=P, j=TILES)
        V.memset(rows[:], 0.0)
        V.memset(p_q_sc[:].bitcast(I32), 0)
        GP.memset(first_tanh[:], 0.0)
        make_identity(nc, ident_b[:])
        make_identity(nc, ident_f[:])
        GP.memset(hd_part[:], 0.0)
        GP.memset(exponents[:, 0:BY_GROUP], -0.5)
        GP.memset(exponents[:, BY_GROUP:], -1.0)
        nc.scalar.dma_start(out=x_sc[:], in_=x_scale.rearrange("(grp r j) q -> r grp (j q)", r=P, j=TILES))
        for j in (0, 2):
            nc.sync.dma_start(out=x_raw[0][:, D * j:D * (j + 2)], in_=x_view[0][:, D * j:D * (j + 2)])
        nc.scalar.dma_start(out=rows[0:NG, 0:GROUP], in_=w.rearrange("(grp f) -> grp f", grp=NG))
        nc.scalar.dma_start(out=rows[NG:2 * NG, 0:GROUP], in_=h.rearrange("(grp f) -> grp f", grp=NG))
        nc.scalar.dma_start(out=rows[0:NM, GROUP:], in_=b.rearrange("(mt c) -> mt c", c=P))
        S.activation(out=first_tanh[:], in_=first_tanh[:], func=ACT.Tanh)
        nc.sync.dma_start(out=x_raw[1][:], in_=x_view[1])
        nc.sync.dma_start(out=p_q[:].bitcast(I32), in_=p_words[0].bitcast(I32))
        for grp in range(2, NG):
            nc.sync.dma_start(out=x_raw[grp][:], in_=x_view[grp])
        nc.sync.dma_start(out=g_raw[0][:], in_=g_view[0])
        for c in range(4):
            nc.sync.dma_start(out=p_q_sc[32 * c:32 * c + 4, :].bitcast(I32), in_=p_scales[0, 4 * c:4 * c + 4, :].bitcast(I32))
        for grp in range(1, NG):
            nc.sync.dma_start(out=g_raw[grp][:], in_=g_view[grp])

        def turn_rows():
            bank = turn_bank([P, TILES + 1, P], BF16, "rows_turned")
            live["rows"] = bank
            for j in range(TILES):
                PE.transpose(bank[:, j, :], rows[:, j:GROUP:TILES], ident_b[:])
            PE.transpose(bank[:, TILES, :], rows[:, GROUP:], ident_b[:])

        def take_rows():
            bank = live["rows"]
            V.tensor_copy(out=wh[:], in_=bank[:, 0:TILES, 0:2 * NG].rearrange("r j c -> r c j"))
            V.tensor_copy(out=h_col[:].rearrange("r (c j) -> r c j", j=TILES), in_=wh[:, NG:, :])
            V.tensor_scalar(out=b_half[:], in0=bank[:, TILES, 0:NM], scalar1=0.5, scalar2=None, op0=ALU.mult)

        def spread_h(grp):
            bank = turn_bank([P, GROUP], F32, "h_spread") if grp < 2 else other_bank([P, GROUP], "h_spread")
            live["h", grp] = bank
            for j in range(TILES):
                column = wh[:, NG + grp, j:j + 1].to_broadcast([P, P])
                PE.matmul(bank[:, P * j:P * (j + 1)], lhsT=column, rhs=ident_b[:], start=True, stop=True)

        def copy_h(grp):
            S.activation(out=h_row[:, GROUP * grp:GROUP * (grp + 1)], in_=live["h", grp][:], func=ACT.Copy, accum_out=ht_part[:, grp:grp + 1])

        def totals():
            V.tensor_reduce(out=ht[:], in_=ht_part[:], axis=AX.X, op=ALU.add)
            GP.tensor_scalar(out=s_sum[:], in0=ht[:], scalar1=1.0, scalar2=2.0 * LAM, op0=ALU.mult, op1=ALU.add)
            GP.tensor_tensor(out=s_inv[:], in0=s_sum[:], in1=exponents[:, BY_GROUP:], op=ALU.pow)
            GP.tensor_scalar(out=s_m2inv[:], in0=s_inv[:], scalar1=-2.0, scalar2=0.0, op0=ALU.mult, op1=ALU.add)
            GP.tensor_scalar(out=s_m1inv[:], in0=s_inv[:], scalar1=-1.0, scalar2=0.0, op0=ALU.mult, op1=ALU.add)
            GP.tensor_scalar(out=e_den[:], in0=ht[:], scalar1=LAM, scalar2=s_sum[:], op0=ALU.add, op1=ALU.mult)
            GP.tensor_tensor(out=e_inv[:], in0=e_den[:], in1=exponents[:, BY_GROUP:], op=ALU.pow)
            GP.tensor_scalar(out=e_fac[:], in0=e_inv[:], scalar1=0.5 * LAM, scalar2=0.0, op0=ALU.mult, op1=ALU.add)

        def total_g(i):
            if i == 0:
                live["gt"] = other_bank([P, T], "gt")
            grp, j = i // TILES, i % TILES
            PE.matmul(live["gt"][:], lhsT=wh[:, grp, j:j + 1].to_broadcast([P, P]), rhs=g_raw[grp][:, j, :], start=i == 0, stop=i == NG * TILES - 1)

        def take_gt():
            S.activation(out=gt_sq[:], in_=live["gt"][:], func=ACT.Square)
            S.activation(out=gt_shift[:], in_=live["gt"][:], func=ACT.Copy, scale=s_m1inv[:])

        def make_last_term():
            V.tensor_scalar(out=last_term[:], in0=gt_sq[:], scalar1=e_fac[:], scalar2=None, op0=ALU.mult)

        def scale_x(grp, j, eng):
            x_bf = handed(("x_bf", grp), lambda: work.tile([P, TILES, D], BF16, name="x_bf", bufs=4, align_bytes=64))
            for q in range(SCALES):
                at = slice(P * q, P * (q + 1))
                values = x_raw[grp][:, D * j + P * q:D * j + P * (q + 1)].bitcast(FP8)
                scale = x_sc[:, grp, SCALES * j + q:SCALES * j + q + 1]
                if eng is V:
                    V.tensor_scalar(out=x_bf[:, j, at], in0=values, scalar1=scale, scalar2=None, op0=ALU.mult)
                else:
                    S.activation(out=x_bf[:, j, at], in_=values, func=ACT.Copy, scale=scale)

        def turn_x(grp, half):
            bank = other_bank([P, 2, 2, P], "x_turned")
            live["x_turned", grp, half] = bank
            for i in range(2):
                words = live["x_bf", grp][:, 2 * half + i, :].bitcast(F32)
                for u in range(2):
                    PE.transpose(bank[:, i, u, :], words[:, u:D // 2:2], ident_f[:])

        def copy_x(grp, half, eng):
            mixed = handed(("x_mixed", grp), lambda: work.tile([P, GROUP * TILES], BF16, name="x_mixed", bufs=3, align_bytes=64))
            words = mixed[:, HALF_GROUP * TILES * half:HALF_GROUP * TILES * (half + 1)].bitcast(F32)
            target = words.rearrange("p (i r u) -> p i r u", i=2, u=2)
            source = live["x_turned", grp, half][:].rearrange("p i u r -> p i r u")
            if eng is V:
                V.tensor_copy(out=target, in_=source)
            else:
                S.copy(out=target, in_=source)

        def quantise_x(grp, c0=0, c1=GROUP):
            V.quantize_mx(out=x_q[:, grp, c0:c1].bitcast(FP8X4), scales=x_q_sc[:, grp, c0:c1], in_=live["x_mixed", grp][:, TILES * c0:TILES * c1])

        def mix_g(grp, eng):
            mixed = work.tile([P, T, TILES], BF16, name="g_mixed", bufs=3, align_bytes=64)
            live["g_mixed", grp] = mixed
            source = g_raw[grp][:].rearrange("r j t -> r t j")
            if eng is V:
                V.tensor_copy(out=mixed[:], in_=source)
            elif eng is GP:
                GP.tensor_scalar(out=mixed[:], in0=source, scalar1=1.0, scalar2=0.0, op0=ALU.mult, op1=ALU.add)
            else:
                S.copy(out=mixed[:], in_=source)

        def quantise_g(grp):
            V.quantize_mx(out=g_q[:, grp, :].bitcast(FP8X4), scales=g_q_sc[:, grp, :], in_=live["g_mixed", grp][:].rearrange("r t j -> r (t j)"))

        def make_z(mt, grp):
            z = z_bank()
            live["z", mt, grp] = z
            PE.matmul_mx(
                out=z[:],
                lhsT=p_q[:, 2 * P * mt:2 * P * (mt + 1)].bitcast(FP4X4),
                lhsT_scale=p_q_sc[:, P * mt:P * (mt + 1)],
                rhs=x_q[:, grp, :].bitcast(FP8X4),
                rhs_scale=x_q_sc[:, grp, :],
                start=True,
                stop=True,
            )

        def make_s(mt, grp):
            s = handed(("s", mt), lambda: work.tile([P, N], F32, name="s", bufs=6, align_bytes=64))
            S.activation(out=s[:, GROUP * grp:GROUP * (grp + 1)], in_=live["z", mt, grp][:], func=ACT.Tanh, bias=b_half[:, mt:mt + 1], scale=0.5)

        def turn_s(mt, grp):
            bank = turn_bank([P, TILES, P], F32, "s_turned")
            live["s_turned", mt, grp] = bank
            for j in range(TILES):
                PE.transpose(bank[:, j, :], live["s", mt][:, GROUP * grp + P * j:GROUP * grp + P * (j + 1)], ident_f[:])

        def weigh_s(mt, grp):
            sw = handed(("sw", mt), lambda: work.tile([P, NG * P * TILES], BF16, name="sw", bufs=6, align_bytes=64))
            V.tensor_tensor(
                out=sw[:, GROUP * grp:GROUP * (grp + 1)].rearrange("r (m j) -> r m j", j=TILES),
                in0=live["s_turned", mt, grp][:].rearrange("r j m -> r m j"),
                in1=wh[:, grp:grp + 1, :].to_broadcast([P, P, TILES]),
                op=ALU.mult,
            )

        def copy_sh(mt, grp):
            sh = handed(("sh", mt), lambda: work.tile([P, N], F32, name="sh", bufs=2, align_bytes=64))
            for j in range(TILES):
                i = TILES * grp + j
                S.activation(out=sh[:, P * i:P * (i + 1)], in_=live["s_turned", mt, grp][:, j, :], func=ACT.Copy, scale=h_col[:, i:i + 1])

        def hd_by_vector(mt, grp0=0, grp1=NG):
            total = hd_part[:, mt, grp0 // 2:grp0 // 2 + 1] if mt < BY_GROUP else hd[:, mt:mt + 1]
            at = slice(GROUP * grp0, GROUP * grp1)
            V.scalar_tensor_tensor(out=product[:, at], in0=live["s", mt][:, at], scalar=1.0, in1=h_row[:, at], op0=ALU.mult, op1=ALU.mult, accum_out=total)

        def hd_by_turns(mt):
            bank = other_bank([P, P], "hd_turned")
            live["hd_turned", mt] = bank
            for i in range(NG * TILES):
                PE.matmul(bank[:], lhsT=live["sh", mt][:, P * i:P * (i + 1)], rhs=ident_f[:], start=i == 0, stop=i == NG * TILES - 1, is_transpose=True)

        def hd_from_turns(mt):
            total = hd_part[:, mt, 0:1] if mt < BY_GROUP else hd[:, mt:mt + 1]
            V.tensor_reduce(out=total, in_=live["hd_turned", mt][:], axis=AX.X, op=ALU.add)

        def join_hd():
            V.tensor_reduce(out=hd[:, 0:BY_GROUP], in_=hd_part[:], axis=AX.X, op=ALU.add)

        def start_den(mt0, mt1):
            V.tensor_scalar(out=den_a[:, mt0:mt1], in0=hd[:, mt0:mt1], scalar1=s_m2inv[:], scalar2=2.0, op0=ALU.mult, op1=ALU.add)

        def make_den(mt0, mt1):
            V.scalar_tensor_tensor(out=den[:, mt0:mt1], in0=hd[:, mt0:mt1], scalar=s_sum[:], in1=den_a[:, mt0:mt1], op0=ALU.add, op1=ALU.mult)

        def root_den(mt0, mt1):
            root = den_root[mt0]
            GP.tensor_tensor(out=root[:, 0:mt1 - mt0], in0=den[:, mt0:mt1], in1=exponents[:, 0:mt1 - mt0], op=ALU.pow)
            for mt in range(mt0, mt1):
                live["root", mt] = root[:, mt - mt0:mt - mt0 + 1]

        def invert_den(mt):
            V.reciprocal(out=den_inv[:], in_=den[:, mt:mt + 1])

        def quantise_sw(mt):
            V.quantize_mx(out=sw_q[mt][:].bitcast(FP8X4), scales=sw_q_sc[mt][:], in_=live["sw", mt][:])

        def make_d(mt, width=T):
            d = other_bank([P, T], "d")
            live["d", mt] = d
            for c0 in range(0, T, width):
                for grp in range(NG):
                    PE.matmul_mx(
                        out=d[:, c0:c0 + width],
                        lhsT=sw_q[mt][:, P * grp:P * (grp + 1)].bitcast(FP8X4),
                        lhsT_scale=sw_q_sc[mt][:, P * grp:P * (grp + 1)],
                        rhs=g_q[:, grp, c0:c0 + width].bitcast(FP8X4),
                        rhs_scale=g_q_sc[:, grp, c0:c0 + width],
                        start=grp == 0,
                        stop=grp == NG - 1,
                    )

        def row_tile(kind, mt):
            return handed((kind, mt), lambda: work.tile([P, T], F32, name=kind, bufs=3))

        def shift_d(mt, c0=0, c1=T):
            V.scalar_tensor_tensor(out=row_tile("shifted", mt)[:, c0:c1], in0=gt_shift[:, c0:c1], scalar=hd[:, mt:mt + 1], in1=live["d", mt][:, c0:c1], op0=ALU.mult, op1=ALU.add)

        def square(mt, c0=0, c1=T):
            scale = 1.0 if mt == LAST else live["root", mt]
            S.activation(out=row_tile("squared", mt)[:, c0:c1], in_=live["shifted", mt][:, c0:c1], func=ACT.Square, scale=scale)

        def store(mt, c0, c1):
            nc.sync.dma_start(out=out[P * mt:P * (mt + 1), c0:c1], in_=live["gain", mt][:, c0:c1])

        def finish(mt, eng):
            eng.tensor_tensor(out=row_tile("gain", mt)[:], in0=live["squared", mt][:], in1=last_term[:], op=ALU.subtract)
            store(mt, 0, T)

        def finish_last(c0, c1):
            gain = row_tile("gain", LAST)
            V.scalar_tensor_tensor(out=gain[:, c0:c1], in0=live["squared", LAST][:, c0:c1], scalar=den_inv[:], in1=last_term[:, c0:c1], op0=ALU.mult, op1=ALU.subtract)
            store(LAST, c0, c1)

        units = [(mt, grp) for grp in range(NG) for mt in range(BY_GROUP)] + [(mt, grp) for mt in range(BY_GROUP, NM) for grp in range(NG)]

        scale_x(0, 0, S)
        scale_x(0, 1, V)
        scale_x(0, 2, V)
        turn_rows()
        scale_x(0, 3, S)
        scale_x(1, 0, S)
        turn_x(0, 1)
        turn_x(0, 0)
        scale_x(1, 2, V)
        scale_x(1, 3, V)
        take_rows()
        spread_h(1)
        copy_x(0, 1, S)
        spread_h(0)
        copy_x(0, 0, S)
        scale_x(2, 3, V)
        scale_x(3, 2, V)
        scale_x(2, 2, V)
        scale_x(2, 0, S)
        scale_x(2, 1, V)
        quantise_x(0)
        scale_x(1, 1, S)
        copy_h(0)
        turn_x(1, 1)
        mix_g(0, V)
        scale_x(3, 1, V)
        scale_x(3, 0, S)
        copy_x(1, 1, S)
        turn_x(1, 0)

        between = {
            -4: [(quantise_g, 0), (turn_x, 2, 1)],
            -3: [(scale_x, 3, 3, S)],
            -2: [(copy_x, 1, 0, V), (turn_x, 2, 0)],
            -1: [(copy_h, 1), (quantise_x, 1)],
            0: [(copy_x, 2, 1, S), (copy_x, 2, 0, V), (turn_x, 3, 0), (mix_g, 1, GP)],
            2: [(quantise_x, 2), (turn_x, 3, 1), (hd_by_vector, 0, 0, 2)],
            3: [(quantise_g, 1)],
            4: [(copy_x, 3, 0, S), (spread_h, 2), (copy_x, 3, 1, S)],
            5: [(total_g, 0), (copy_h, 2)],
            6: [(quantise_x, 3), (total_g, 1), (total_g, 2)],
            7: [(total_g, 3), (spread_h, 3), (hd_by_vector, 1, 0, 2)],
            8: [(mix_g, 2, GP)],
            9: [(copy_h, 3)],
            10: [(totals,), (total_g, 4)],
            11: [(total_g, 5), (total_g, 6)],
            12: [(total_g, 7), (hd_by_vector, 1, 2, 4), (total_g, 8), (total_g, 9), (quantise_sw, 0)],
            13: [(mix_g, 3, S)],
            14: [(total_g, 10), (quantise_sw, 1), (total_g, 11), (hd_by_vector, 3), (total_g, 12), (total_g, 13), (total_g, 14)],
            15: [(total_g, 15), (hd_by_vector, 0, 2, 4), (quantise_g, 3), (take_gt,)],
            16: [(hd_by_turns, 2), (quantise_g, 2)],
            17: [(hd_from_turns, 2), (make_d, 0), (make_last_term,), (join_hd,)],
            18: [(start_den, 0, 4), (quantise_sw, 3)],
            19: [(make_d, 1)],
            20: [(quantise_sw, 2), (quantise_sw, 4)],
            21: [(make_den, 0, 4), (shift_d, 1), (root_den, 0, 4), (shift_d, 0)],
            22: [(square, 0), (make_d, 2)],
            23: [(hd_by_vector, 5), (square, 1), (hd_by_turns, 4)],
            24: [(hd_from_turns, 4), (make_d, 3), (shift_d, 2), (square, 2), (make_d, 4), (quantise_sw, 5)],
            25: [(finish, 0, GP), (finish, 2, GP), (start_den, 4, 6), (make_den, 4, 6)],
            26: [(root_den, 4, 6), (shift_d, 3), (make_d, 5), (finish, 1, GP), (shift_d, 4), (square, 3)],
            27: [(square, 4), (hd_by_turns, 6)],
            28: [(finish, 3, V), (quantise_sw, 6), (shift_d, 5)],
            30: [(hd_from_turns, 6)],
        }

        for i in range(-4, len(units)):
            pair = (i, i + 1) if i % 2 == 0 else ()
            for k in pair:
                if k + 4 < len(units):
                    make_z(*units[k + 4])
            if 0 <= i + 3 < len(units):
                make_s(*units[i + 3])
            for k in pair:
                if 0 <= k + 1 < len(units):
                    turn_s(*units[k + 1])
            if i >= 0:
                mt, grp = units[i]
                weigh_s(mt, grp)
                if mt in TURNED:
                    copy_sh(mt, grp)
            for piece in between.get(i, ()):
                piece[0](*piece[1:])

        start_den(6, 7)
        quantise_sw(7)
        hd_by_vector(7)
        make_den(6, 7)
        start_den(7, 8)
        make_d(6)
        square(5)
        finish(4, GP)
        finish(5, GP)
        make_d(LAST, T // 2)
        shift_d(LAST, 0, T // 2)
        make_den(7, 8)
        square(LAST, 0, T // 2)
        shift_d(6)
        invert_den(LAST)
        shift_d(LAST, T // 2, T)
        root_den(6, 7)
        square(6)
        finish_last(0, T // 2)
        finish(6, V)
        square(LAST, T // 2, T)
        finish_last(T // 2, T)
